import numpy as np, ml_dtypes
CORES = [2,3,42,43,82,83,122,123]
N = 8
import mx_ref
BF = ml_dtypes.bfloat16
def gentries(a):
    return np.ascontiguousarray(a.reshape(8, 16, -1).transpose(0, 2, 1)).reshape(8, -1)
def gtable(e):
    e = np.asarray(e); return np.ascontiguousarray(e.reshape(8, -1, 16).transpose(0, 2, 1)).reshape(128, -1).astype(np.int32)
def gcols(t, e):
    v = np.concatenate([t.reshape(8, 16, -1, 4), np.zeros((8, 16, 1, 4), BF)], axis=2)
    return np.ascontiguousarray(np.stack([v[g][:, e[g]] for g in range(8)])).reshape(128, -1)
def gpick(z, e):
    return np.concatenate([z[16 * g:16 * g + 16][:, e[g]] for g in range(8)])
def tile(rs):
    return np.stack(rs, axis=2).reshape(128, -1).astype(BF)
def pick(q, e):
    c = np.concatenate([q[0].reshape(128, -1, 4), np.zeros((128, 1, 4), np.uint8)], axis=1); s = np.concatenate([q[1], np.ones((16, 1), np.uint8)], axis=1)
    return (np.ascontiguousarray(c[:, e].reshape(128, -1)), np.ascontiguousarray(s[:, e]))
def join(*qs):
    return (np.concatenate([q[0] for q in qs], axis=1), np.concatenate([q[1] for q in qs], axis=1))
def put(q, e, v):
    c, s = q[0].reshape(128, -1, 4).copy(), q[1].copy(); c[:, e] = v[0].reshape(128, -1, 4); s[:, e] = v[1]
    return (c.reshape(128, -1), s)
def pk(c, s):
    return (np.ascontiguousarray(c), mx_ref.live(s))
def emit(q):
    return q[0], q[1]
def packed(v, rng):
    q = [mx_ref.quantize(np.ascontiguousarray(v[r])) for r in range(N)]
    return np.stack([a for a, b in q]), np.stack([mx_ref.plane(b, rng) for a, b in q])
def values_of_codes():
    e, c = np.zeros((128, 128, 4), np.float32), np.zeros((128, 2, 4), np.uint8)
    e[np.arange(128), np.arange(128), 0] = 1
    c[:127, :, 0] = np.arange(256).reshape(2, 128).T[:127]
    return mx_ref.matmul(mx_ref.quantize(e.reshape(128, 512).astype(BF)), (c.reshape(128, 8), np.full((16, 2), 127, np.uint8))).T.reshape(-1).astype(np.float64)
CODE_VALUE, SCALE_VALUE = values_of_codes(), 2.0 ** (np.arange(256) - 127.0)
def decode(q):
    return (CODE_VALUE[q[0]].reshape(16, 8, -1, 4) * SCALE_VALUE[q[1]][:, None, :, None] + 0.0).reshape(128, -1).astype(np.float32)
def f(rng, *shape):
    return mx_ref.flush((rng.standard_normal(shape, dtype=np.float32) * np.exp2(rng.integers(-2, 3, shape[:-1] + (1,)))).astype(BF))
def wide(rng, *shape, cols=0):
    v = rng.standard_normal(shape, dtype=np.float32) * np.exp2(rng.integers(-12, 13, shape)).astype(np.float32)
    if cols: v *= np.repeat(np.exp2(rng.integers(-cols, cols + 1, shape[:-2] + (1, shape[-1] // 4))) * (rng.random(shape[:-2] + (1, shape[-1] // 4)) > 0.0625), 4, axis=-1).astype(np.float32)
    return mx_ref.flush(v.astype(BF))
C = 320
STEP = [1, 2, 4]
GROUP, PLACE = np.arange(8)[:, None], np.arange(C)
def numbers_of(rng):
    return {"x": np.array(f(rng, N, 128, 4 * C)), "u": np.array(f(rng, N, 128, 512)), "v": np.array(f(rng, N, 128, 512))}
def orders(rng):
    return rng.permuted(np.tile(np.arange(C), (N, 8, 1)), axis=2)
def paired(e):
    k = np.zeros_like(e)
    np.put_along_axis(k, e[:, :, 0::2], e[:, :, 1::2], 2)
    np.put_along_axis(k, e[:, :, 1::2], e[:, :, 0::2], 2)
    return k
def stored(p, q, mu):
    return {a: np.stack([gtable(k[r]) for r in range(N)]) for a, k in (("pl", p), ("ql", q), ("ml", mu))}
def lists(rng):
    return stored(paired(orders(rng)), paired(orders(rng)), paired(orders(rng)))
def layers(rng, still=[]):
    w = np.array(f(rng, N, 128, 2048)).reshape(N, 8, 16, 4, 8, 16, 4)
    for i in still:
        w[:, :, i] = 0
        w[:, :, :, :, :, i] = 0
    return w
def weights(rng, w):
    c, s = packed(np.ascontiguousarray(w).reshape(N, 128, 2048), rng)
    return {"wc": c, "ws": s}
def setup_inputs(rng):
    return {**numbers_of(rng), **lists(rng), **weights(rng, layers(rng))}
def setup_inputs_ties(rng):
    d = numbers_of(rng)
    e = orders(rng)
    mu = paired(orders(rng))
    k = np.zeros((N, 8, C))
    for r in range(N):
        h = rng.permutation(8)
        c = rng.integers(0, C, 2)
        k[r, h[1], min(c[0], mu[r, h[1], c[0]])] = -1
        k[r, h[2], max(c[1], mu[r, h[2], c[1]])] = -1
        k[r, h[3], e[r, h[3], :2]] = -1
        k[r, h[4]] = rng.integers(-4, 0, C)
        k[r, h[5]] = rng.integers(-1, 3, C)
        k[r, h[6]] = rng.integers(1, 4, C)
        k[r, h[7]] = rng.integers(0, 2, C)
        k[r, h[7], e[r, h[7], 0]] = -1
        k[r, h[7], e[r, h[7], 2 * rng.integers(1, C // 2)]] = -1
    x = d["x"].reshape(N, 8, 16, C, 4)
    x[:, :, 0] = 0
    x[:, :, 0, :, 0] = k.astype(np.float32).astype(BF)
    u = d["u"].reshape(N, 128, 128, 4)
    u[:, :, ::16] = 0
    for h in range(0, 128, 16): u[:, h, h, 0] = 1
    return {"x": x.reshape(N, 128, 4 * C), "u": u.reshape(N, 128, 512), "v": d["v"], **stored(paired(e), paired(np.roll(e, -1, axis=2)), mu), **weights(rng, layers(rng, [0]))}
def setup_inputs_near(rng):
    d = numbers_of(rng)
    x = d["x"].astype(np.float32).reshape(N, 8, 16, C, 4)
    x[:, :, :2] = 0
    x[:, :, 8:] = 0
    x[:, :, 1, :, 0] = rng.choice([-1.0, 1.0], (N, 8, C)) * (1.0 + 0.125 * rng.integers(0, 8, (N, 8, C))) * 2.0 ** -7
    u = d["u"].reshape(N, 128, 128, 4)
    u[:, :, ::16] = 0
    w = layers(rng, [0, 1, 8, 9, 10, 11, 12, 13, 14, 15])
    o = rng.permutation(N) % 4
    for r in range(N):
        c = rng.choice([-1.0, 1.0], (8, 1))
        s = rng.integers(0, 16, (8, C))
        digits = ((s[:, :, None] >> np.arange(4)) & 1) * np.exp2(np.arange(4) - 23.0)
        if o[r] < 2:
            x[r, :, 0, :, 0] = c
            x[r, :, 8] = digits
            x[r, :, 11, :, 0] = 2.0 ** -10
        elif o[r] == 2: x[r, :, 8] = digits * rng.choice([-1.0, 1.0], (8, C, 1))
        else:
            x[r, :, 8, :, 0] = np.where(s < 8, 1.25, 0.0) * 2.0 ** -29 * c
            x[r, :, 9, :, 0] = np.where(s < 8, 0.0, 1.125) * 2.0 ** -29 * c
            x[r, :, 12, :, 0] = 2.0 ** -28
            for g in range(8): w[r, g, 1, 0, g, 10, 0] = 2.0 ** -30
            for i, g in enumerate(rng.permutation(8)[:4]):
                if i < 2:
                    e = rng.choice([-1.0, 1.0], C) * 2.0 ** -29
                    x[r, g, 8, :, 0] = 1.25 * e
                    x[r, g, 9, :, 0] = -1.125 * e
                else:
                    x[r, g, 8:] = 0
                    x[r, g, 12, :, 0] = 2.0 ** -30
                    w[r, g, 1, 0, g, 10, 0] = -2.0 ** -30
                    w[r, g, 1, 0, g, 11, 0] = 2.0 ** -30
        at = [0, C - 1, int(rng.integers(C)), int(rng.integers(C))]
        for g, j in zip(rng.permutation(8)[:4], at): x[r, g, 0, j, 0] = 2.0 ** 29 * rng.choice([-1.0, 1.0])
        k = 1.0 if o[r] == 0 else 2.0 ** -30
        for h in range(0, 128, 16):
            u[r, h, h, 0] = k if o[r] < 2 else 1.0
            if o[r] < 2: u[r, h + 11, h, 0] = k
            if o[r] < 3: u[r, h + 8, h] = k
            else:
                u[r, h + 8, h, 0] = k
                u[r, h + 9, h, 0] = 1.125 * k
                u[r, h + 10, h, 0] = k
                u[r, h + 11, h, 0] = 1.125 * k
    return {"x": x.reshape(N, 128, 4 * C).astype(BF), "u": u.reshape(N, 128, 512), "v": d["v"], **lists(rng), **weights(rng, w)}
def setup_inputs_odd(rng):
    d = numbers_of(rng)
    x = (1.0 + (2 * rng.integers(0, 64, (N, 16, 8, C, 4)) + 1) * 2.0 ** -7) * np.exp2(-rng.integers(0, 7, (N, 16, 8, C, 4)).astype(np.float64)) * rng.choice([-1.0, 1.0], (N, 16, 8, C, 4))
    x[:, :, 0, :, 0] = 1.96875 * 2.0 ** 8 * rng.choice([-1.0, 1.0], (N, 16, C))
    x[:, 1::2, 0, :, 0] *= np.where(rng.random((N, 8, C)) < 0.5, 2.0 ** -6, 1.0)
    u = d["u"].reshape(N, 16, 8, 128, 4)
    u[:, :, 0, ::16] = 0
    for r in range(N):
        for i, g in enumerate(rng.permutation(8)[:4]):
            x[r, 2 * g, 1, :, 0] = (8 + rng.integers(0, 2, C)) * 2.0 ** (i - 8)
            u[r, :, :, 16 * g] = 0
            u[r, 2 * g, 1, 16 * g, 0] = 1.0
    return {"x": x.astype(np.float32).reshape(N, 128, 4 * C).astype(BF), "u": u.reshape(N, 128, 512), "v": d["v"], **lists(rng), **weights(rng, layers(rng, [0, 8]))}
def setup_inputs_ends(rng):
    d = numbers_of(rng)
    o, e = rng.permutation(N) % 2, rng.permutation(N) % 4
    sign = rng.choice([-1.0, 1.0], (128, 1, 4))
    half = np.repeat(rng.choice([0.5, 1.0], (N, 1, C, 2)), 2, axis=3)
    small = sign * (1.0 + 0.125 * rng.integers(0, 8, (N, 128, C, 4))) * 2.0 ** -30
    x = sign * half * (14 + rng.integers(0, 3, (N, 128, C, 4))) * 2.0 ** 26
    x[o == 1] = small[o == 1]
    x[:, 112:120] = sign[112:120]
    x[:, 120:] = small[:, 120:]
    size = np.where(o == 0, 2.0 ** 30, 2.0 ** -30)
    kinds = np.array([[1, 1, 1, 1]] * 2 + [[-1, -1, -1, -1]] * 3 + [[1, 1, -1, -1]] * 2 + [[0, 0, 0, 0]])
    u = d["u"].astype(np.float32).reshape(N, 128, 128, 4)
    for r in range(N): u[r, :, ::16] = sign * kinds[rng.permutation(8)][None] * size[r]
    u[:, 112:, ::16] = 0
    v = rng.choice([-1.0, 1.0], (N, 128, 512)) * size[:, None, None]
    a = orders(rng)
    p, q, mu = paired(a), paired(np.roll(a, -1, axis=2)), paired(orders(rng))
    q[e == 1] = p[e == 1]
    mu[e == 1] = p[e == 1]
    p[e == 2] = C - 1 - np.arange(C)
    q[e == 2] = np.arange(C) ^ 1
    q[e == 3] = paired(orders(rng))[e == 3]
    w = np.zeros((N, 128, 4, 128, 4), np.float32)
    i, n = np.arange(112), np.arange(8)
    for b in range(4):
        for r in range(N):
            if o[r] == 0: w[r, i, b, i, b] = -4.0
            w[r, (120 if b < 2 else 96) + n, b, 112 + n, b] = 2.0 ** 30 if b < 2 else 2.0 ** -30
    return {"x": x.astype(np.float32).reshape(N, 128, 4 * C).astype(BF), "u": u.reshape(N, 128, 512).astype(BF), "v": v.astype(np.float32).astype(BF), **stored(p, q, mu), **weights(rng, w.astype(BF))}
def setup_inputs_spread(rng):
    d = setup_inputs(rng)
    d["x"] = wide(rng, N, 128, 4 * C, cols=6)
    return d
def check_inputs(d):
    b = []
    for k in ("x", "u", "v"):
        a = np.abs(d[k].astype(np.float32))
        if not (np.isfinite(a).all() and ((a == 0) | (a >= 2.0 ** -30) & (a <= 2.0 ** 30)).all()): b.append("a value of " + k)
    for k in ("pl", "ql", "ml"):
        for r in range(N):
            e = gentries(d[k][r])
            if not ((e >= 0) & (e < C)).all(): b.append("an entry of " + k)
            elif (e == PLACE).any() or (e[GROUP, e] != PLACE).any(): b.append(k + ": no involution without fixed points")
    none, least, most = [emit(mx_ref.quantize(np.full((128, 16), k, np.float32).astype(BF)))[1][0, 0] for k in (0.0, 2.0 ** -30, 2.0 ** 30)]
    for r in range(N):
        if ((d["wc"][r] == 0x7F) | (d["wc"][r] == 0xFF)).any(): b.append("wc: a code that is no number")
        s = mx_ref.live(d["ws"][r])
        if ((s != none) & ((s < least) | (s > most))).any(): b.append("ws: a scale out of range")
        if (((d["wc"][r].reshape(16, 8, 512, 4) & 0x7F) != 0) & (s == none)[:, None, :, None]).any(): b.append("wc: a code other than zero under the scale of zeros")
    return b
def powers(a):
    k = [np.tile(PLACE, (8, 1))]
    for i in range(C // 2 - 1): k.append(a[GROUP, k[-1]])
    return np.stack(k)
def mirror(p, q, stop):
    ahead, back = powers(q[GROUP, p]), powers(p[GROUP, q])
    i, j = np.argmax(stop[GROUP, ahead], axis=0), np.argmax(stop[GROUP, back], axis=0)
    return ahead[i, GROUP, back[j, GROUP, PLACE]]
def reference(x, u, v, pl, ql, ml, wc, ws):
    qu = [mx_ref.quantize(u[r]) for r in range(N)]
    lay = [pk(wc[r], ws[r]) for r in range(N)]
    p, q, mu = [[gentries(a[r]).astype(np.int64) for r in range(N)] for a in (pl, ql, ml)]
    now = [x[r] for r in range(N)]
    for step in STEP:
        own, sent, image = [], [], []
        for r in range(N):
            t = mx_ref.quantize(now[r])
            s = mx_ref.matmul(qu[r], t)[::16] + np.float32(0.0)
            d = decode(t).astype(BF)
            m = mirror(p[r], q[r], s < 0)
            z = (gcols(d, m).astype(np.float32) + gcols(d, q[r][GROUP, p[r]]).astype(np.float32)) * np.float32(0.5)
            sent.append(mx_ref.quantize(z.astype(BF)))
            w = (PLACE < mu[r]) & (s[GROUP, m] > s[GROUP, m[GROUP, mu[r]]])
            e = np.where(w | w[GROUP, mu[r]], mu[r], PLACE)
            q[r] = e[GROUP, q[r][GROUP, e]]
            own.append(d)
            image.append(m)
        now = [tile([gpick(mx_ref.matmul(pick(lay[r], np.arange(128 * b, 128 * b + 128)), sent[r ^ step]) * np.float32(0.03125), image[r]) + own[r][:, b::4].astype(np.float32) for b in range(4)]) for r in range(N)]
    y, qo = np.zeros((N, 128, C), np.float32), np.zeros((N, 8, C), np.float32)
    oc, osc = np.zeros((N, 128, 4 * C), np.uint8), np.zeros((N, 16, C), np.uint8)
    for r in range(N):
        t = mx_ref.quantize(now[r])
        y[r] = mx_ref.matmul(mx_ref.quantize(v[r]), t)
        qo[r] = q[r]
        oc[r], osc[r] = emit(t)
    return {"y": y, "qo": qo, "oc": oc, "osc": osc}

@@ -1,0 +1,440 @@
+from concourse.bass import DstId, RemoteDMATransfer
+from concourse.mybir import dt, AluOpType as OP, ActivationFunctionType as AF
+
+C = 320
+K = C // 16
+STEP = [1, 2, 4]
+STAGES = [3, 3, 3, 3, 2]
+BIG = 1024.0
+SLOPE, SHIFT = 164, -51997
+HALF = 512
+UNMET = 162
+NCELL = 53000
+
+
+def wide(*names):
+    return {n: ("sbuf", [128, C], "float32") for n in names}
+
+
+def double(*names):
+    return {n: ("sbuf", [128, 2 * C], "float32") for n in names}
+
+
+def small(d, *names):
+    return {n: ("sbuf", [128, K], d) for n in names}
+
+
+def column(d, *names):
+    return {n: ("sbuf", [128, 1], d) for n in names}
+
+
+def tiles(*names):
+    return {n: ("sbuf", [128, 4 * C], "bfloat16") for n in names}
+
+
+def codes(n, *pairs):
+    d = {}
+    for c, s in pairs:
+        d[c] = ("sbuf", [128, n], "float8_e4m3fn_x4")
+        d[s] = ("sbuf", [128, n], "uint8")
+    return d
+
+
+SCRATCH = {
+    **tiles("x0", "xn", "zt", "fo", "fh", "fa"),
+    "ut": ("sbuf", [128, 512], "bfloat16"), "vt": ("sbuf", [128, 512], "bfloat16"),
+    **codes(128, ("uc", "us"), ("urc", "urs"), ("vc", "vs")), **codes(512, ("lc", "ls"), ("ec", "es")),
+    **codes(C, *[("zc%d" % r, "zs%d" % r) for r in range(3)], *[("ac%d" % r, "as%d" % r) for r in range(3)], *[("tc%d" % r, "ts%d" % r) for r in range(4)]),
+    "eone": ("sbuf", [128, 516], "bfloat16"), "ebase": ("sbuf", [128, 516], "bfloat16"),
+    "qpi": ("sbuf", [128, C], "int32"), "mpi": ("sbuf", [128, C], "int32"), "ji": ("sbuf", [128, C], "int32"), "ja": ("sbuf", [128, C], "int32"),
+    "u8i": ("sbuf", [128, 8], "int32"), "upick": ("sbuf", [128, 8], "uint16"), "cb": ("sbuf", [128, C], "bfloat16"),
+    "fm": ("sbuf", [128, 2 * C], "bfloat16"), "y3": ("sbuf", [128, 2 * C], "bfloat16"),
+    **column("int32", "pi1", "pa1"), **column("float32", "pf1", "p20", "qoff", "nqo", "nwg", "nqh"),
+    **small("int32", "pli", "mli", "k16", "k1"),
+    **small("uint16", "pu", "mu16", "lowu", "highu", "piu", "ppu", "qpu", "wu", "wz", "lu", "k1u", "k2u", "sgu", "qsu"),
+    **small("uint16", *["%s%d" % (n, r) for n in ("am", "aa", "mo", "ao") for r in range(3)]),
+    **small("float32", "coff", "c640", "chalf", "nf", "nfk", "wf", "wg", "gg", "df", "t1", "t2", "t3", "t4", "t5"),
+    **wide("md", "lg", "aw", "f320", "ssb", "sc0", "sc1", "sc2", "mw", "sm", "smh", "sw", "sgw", "qs"),
+    **double("wa", "wb", "d1", "d2", "d3"), **{n: ("sbuf", [128, HALF + C], "float32") for n in ("qq", "qr", "cm")},
+    "lw": ("sbuf", [128, 3 * C], "float32"), "tab": ("sbuf", [128, NCELL], "bfloat16"), "rs": ("sbuf", [128, 3 * C], "float32"),
+    "pa": ("psum", [128, 2048], "float32"), "pb": ("psum", [128, 2048], "float32"),
+}
+
+SEMAPHORES = ["qV", "qS", "qT", "qG", "sent", "stored"] + ["ld_" + n for n in ("x", "u", "v", "wc", "ws", "pl", "ml", "qw", "mw")]
+for _r in range(3):
+    SEMAPHORES += ["arX%d" % _r, "arA%d" % _r, "arM%d" % _r]
+
+
+def make_queues(g, T):
+    queues = {"V": g.vector, "S": g.scalar, "T": g.tensor, "G": g, "Y": g.sync}
+    count = {"V": 0, "S": 0, "T": 0, "G": 0}
+    clocks = {}
+    known = {q: {} for q in queues}
+    writer, readers = {}, {}
+
+    def merge(a, b):
+        for k, n in b.items():
+            if a.get(k, 0) < n:
+                a[k] = n
+
+    def need(q, sem, n):
+        if known[q].get(sem, 0) >= n:
+            return
+        queues[q].wait_ge(T.sem[sem], n)
+        if (sem, n) in clocks:
+            merge(known[q], clocks[(sem, n)])
+        known[q][sem] = n
+
+    def waits(q, reads, writes):
+        own = "q" + q
+        want = {}
+        for k in reads:
+            if k in writer:
+                s, n = writer[k]
+                want[s] = max(want.get(s, 0), n)
+        for k in writes:
+            if k in writer:
+                s, n = writer[k]
+                want[s] = max(want.get(s, 0), n)
+            for s, n in readers.get(k, {}).items():
+                if s != own:
+                    want[s] = max(want.get(s, 0), n)
+        for s, n in want.items():
+            need(q, s, n)
+
+    def note(sem, n, reads, writes):
+        for k in reads:
+            r = readers.setdefault(k, {})
+            r[sem] = max(r.get(sem, 0), n)
+        for k in writes:
+            writer[k] = (sem, n)
+            readers[k] = {}
+
+    def op(q, fn, reads, writes):
+        waits(q, reads, writes)
+        inst = fn(queues[q])
+        count[q] += 1
+        sem = "q" + q
+        inst.then_inc(T.sem[sem], 1)
+        c = dict(known[q])
+        merge(c, clocks.get((sem, count[q] - 1), {}))
+        c[sem] = count[q]
+        clocks[(sem, count[q])] = c
+        note(sem, count[q], reads, writes)
+
+    def dma(q, pairs, sem, total, reads, writes):
+        waits(q, reads, writes)
+        for out, in_ in pairs:
+            queues[q].dma_start(out, in_).then_inc(T.sem[sem], 16)
+        note(sem, total, reads, writes)
+
+    def arrives(sem, total, writes):
+        note(sem, total, [], writes)
+
+    return op, dma, arrives, waits, need, count
+
+
+def rank_program(g, core, T, topo):
+    rank = T.rank_of(core)
+    if rank is None:
+        return
+    op, dma, arrives, waits, need, count = make_queues(g, T)
+    sent = [0]
+
+    def send(dst, out, in_, sem, key):
+        waits("G", [key], [])
+        rid, pid, _ = topo.addr(dst)
+        g.remote_dma(out, in_, T.sem[sem], T.sem.sent, pid, rid, topo.mask(core, dst))
+        sent[0] += len(topo.engines(core, dst))
+
+    def copy(q, out, in_, reads, writes, scale=None):
+        if q == "S":
+            if scale is None:
+                op("S", lambda e: e.activation(out, in_, AF.Copy), reads, writes)
+            else:
+                op("S", lambda e: e.activation(out, in_, AF.Copy, 0.0, scale), reads, writes)
+        else:
+            op("V", lambda e: e.tensor_copy(out, in_), reads, writes)
+
+    def tt(out, a, b, o, reads, writes):
+        op("V", lambda e: e.tensor_tensor(out, a, b, o), reads, writes)
+
+    def ts(out, a, s1, o1, reads, writes, s2=None, o2=None):
+        if o2 is None:
+            op("V", lambda e: e.tensor_scalar(out, a, s1, None, o1), reads, writes)
+        else:
+            op("V", lambda e: e.tensor_scalar(out, a, s1, s2, o1, o2), reads, writes)
+
+    def fill(ap, value, key):
+        op("V", lambda e: e.memset(ap, value), [], [key])
+
+    def ind(win, off, a=0, b=C):
+        return T[win][:, a:b].indirect(T[off][:, 0:K])
+
+    def scan(dst, src):
+        op("V", lambda e: e.tensor_tensor_scan(T[dst][:], T.md[:], T[src][:, 0:C], 0.0, OP.add, OP.max), ["md", src], [dst])
+
+    def ends(sc):
+        return T[sc][:, 15:C:16]
+
+    def take(out, sc, extra=None, o=None):
+        ts(T[out][:], ends(sc), T.qoff[:, 0:1], OP.subtract, [sc, "qoff"], [out], extra, o)
+
+    def mm(bank, lc, ls, rc, rs, reads, a):
+        buf, b = bank
+        op("T", lambda e: e.matmul_mx(T[buf][:, 512 * b:512 * b + C], T[lc][:, a:a + 128], T[ls][:, a:a + 128], T[rc][:], T[rs][:], True, True), reads, [(buf, b)])
+
+    def quant(c, s, t, keys=None):
+        op("V", lambda e: e.quantize_mx(T[c][:], T[s][:], T[t][:]), keys or [t], [c, s])
+
+    def unit(b):
+        op("V", lambda e: e.quantize_mx(T.ec[:, 128 * b:128 * b + 128], T.es[:, 128 * b:128 * b + 128], T.ebase[:, 3 - b:515 - b]), ["ebase"], [("ec", b)])
+
+    dma("S", [(T.ut[:], T.u[:])], "ld_u", 16, [], ["ut"])
+    dma("S", [(T.x0[:], T.x[:])], "ld_x", 16, [], ["x0"])
+    dma("S", [(T.pli[:], T.pl[:])], "ld_pl", 16, [], ["pli"])
+    dma("S", [(T.mli[:], T.ml[:])], "ld_ml", 16, [], ["mli"])
+    dma("Y", [(T.qpi[i:128:16, :], T.ql[:]) for i in range(16)], "ld_qw", 256, [], ["qpi"])
+    need("Y", "ld_x", 16)
+    dma("Y", [(T.lc[:].bitcast(dt.uint8), T.wc[:])], "ld_wc", 16, [], ["lc"])
+    dma("Y", [(T.ls[:], T.ws[:])], "ld_ws", 16, [], ["ls"])
+    dma("Y", [(T.mpi[i:128:16, :], T.ml[:]) for i in range(16)], "ld_mw", 256, [], ["mpi"])
+    dma("Y", [(T.vt[:], T.v[:])], "ld_v", 16, [], ["vt"])
+    for r in range(3):
+        e = len(topo.engines(T.cores[rank ^ STEP[r]], core))
+        arrives("arX%d" % r, 2 * e, ["ac%d" % r, "as%d" % r])
+        arrives("arA%d" % r, e, ["aa%d" % r])
+        arrives("arM%d" % r, e, ["am%d" % r])
+
+    def iota(name, a, b, step, base, mult, flag=False):
+        op("G", lambda e: e.iota(T[name][:, a:b], [[step, b - a]], base, mult, allow_small_or_imprecise_dtypes=True) if flag else e.iota(T[name][:, a:b], [[step, b - a]], base, mult), [], [name])
+    iota("pi1", 0, 1, 1, 0, 1)
+    iota("ji", 0, C, 1, 4096, -1)
+    iota("u8i", 0, 8, 16, 0, 0)
+    iota("k1", 0, K, 1, 0, 0)
+    iota("k16", 0, K, 16, 0, 0)
+    fill(T.eone[:], 1.0, "eone")
+    op("G", lambda e: e.affine_select(T.ebase[:], T.eone[:], [[-1, 516]], OP.is_equal, 0.0, 3, 4), ["eone"], ["ebase"])
+    iota("wa", C, 2 * C, 1, C, 0, True)
+    iota("wb", C, 2 * C, 1, C, 0, True)
+    iota("cb", 0, C, 1, -160, 0, True)
+    iota("cm", 0, C, 1, 0, 0, True)
+    ts(T.pa1[:], T.pi1[:], 15, OP.bitwise_and, ["pi1"], ["pa1"])
+    fill(T.d1[:, C:2 * C], 0.0, "d1")
+    ts(T.pf1[:], T.pa1[:], 1.0, OP.mult, ["pa1"], ["pf1"])
+    ts(T.ja[:], T.ji[:], 15, OP.bitwise_and, ["ji"], ["ja"])
+    ts(T.p20[:], T.pf1[:], 20.0, OP.mult, ["pf1"], ["p20"])
+    ts(T.qoff[:], T.pf1[:], -BIG, OP.mult, ["pf1"], ["qoff"], 15 * BIG, OP.add)
+    ts(T.nqo[:], T.pf1[:], BIG, OP.mult, ["pf1"], ["nqo"], -15 * BIG, OP.add)
+    ts(T.sc2[:], T.ja[:], 0.0, OP.is_equal, ["ja"], ["sc2"], -33 * BIG, OP.mult)
+    copy("V", T.upick[:], T.u8i[:], ["u8i"], ["upick"])
+    ts(T.piu[:], T.k1[:], T.p20[:, 0:1], OP.add, ["k1", "p20"], ["piu"])
+    ts(T.coff[:], T.k16[:], T.pf1[:, 0:1], OP.add, ["k16", "pf1"], ["coff"])
+    ts(T.md[:], T.sc2[:], BIG, OP.add, ["sc2"], ["md"])
+    ts(T.nwg[:], T.nqo[:], float(SLOPE), OP.mult, ["nqo"], ["nwg"], float(SHIFT), OP.add)
+    ts(T.c640[:], T.coff[:], float(2 * C), OP.add, ["coff"], ["c640"])
+    ts(T.chalf[:], T.coff[:], 1.0 / HALF, OP.mult, ["coff"], ["chalf"])
+    ts(T.nqh[:], T.nqo[:], float(HALF), OP.mult, ["nqo"], ["nqh"])
+    ts(T.k16[:], T.pli[:], 15, OP.bitwise_and, ["pli"], ["k16"])
+    ts(T.k1[:], T.pli[:], 4, OP.arith_shift_right, ["pli"], ["k1"])
+    copy("V", T.pu[:], T.pli[:], ["pli"], ["pu"])
+    ts(T.t1[:], T.k16[:], 20.0, OP.mult, ["k16"], ["t1"])
+    fill(T.lw[:, 0:C], float(2 * UNMET), "lw")
+    for n in ("d2", "d3"):
+        copy("S", T[n][:, C:2 * C], T.d1[:, C:2 * C], ["d1"], [n])
+
+    tt(T.t2[:], T.t1[:], T.k1[:], OP.add, ["t1", "k1"], ["t2"])
+    quant("uc", "us", "ut")
+    copy("V", T.ppu[:], T.t2[:], ["t2"], ["ppu"])
+    op("S", lambda e: e.activation(T.urs[:], T.us[:].indirect(T.upick[:, 0:8]), AF.Copy), ["us", "upick"], ["urs"])
+    op("V", lambda e: e.tensor_copy(T.urc[:].bitcast(dt.uint32), T.uc[:].bitcast(dt.uint32).indirect(T.upick[:, 0:8])), ["uc", "upick"], ["urc"])
+    copy("V", T.gg[:], T.mli[:], ["mli"], ["gg"])
+    copy("V", T.mu16[:], T.mli[:], ["mli"], ["mu16"])
+    tt(T.wf[:], T.gg[:], T.coff[:], OP.min, ["gg", "coff"], ["wf"])
+    tt(T.wg[:], T.gg[:], T.coff[:], OP.max, ["gg", "coff"], ["wg"])
+    quant("tc0", "ts0", "x0")
+    copy("V", T.lowu[:], T.wf[:], ["wf"], ["lowu"])
+    copy("V", T.highu[:], T.wg[:], ["wg"], ["highu"])
+    copy("S", T.aw[:], ind("qpi", "ppu"), ["qpi", "ppu"], ["aw"])
+    copy("S", T.qq[:, 0:C], ind("qpi", "piu"), ["qpi", "piu"], ["qq"])
+    unit(0)
+    scan("sc0", "aw")
+
+    qcur, qnew = "qq", "qr"
+    for r in range(3):
+        partner = T.cores[rank ^ STEP[r]]
+        tc, tsn, zc, zs = "tc%d" % r, "ts%d" % r, "zc%d" % r, "zs%d" % r
+        ao, mo, aa, am, ac, asn = "ao%d" % r, "mo%d" % r, "aa%d" % r, "am%d" % r, "ac%d" % r, "as%d" % r
+        send(partner, T[ac][:].bitcast(dt.uint8), T[tc][:].bitcast(dt.uint8), "arX%d" % r, tc)
+        send(partner, T[asn][:], T[tsn][:], "arX%d" % r, tsn)
+        mm(("pb", 0), "urc", "urs", tc, tsn, ["urc", "urs", tc, tsn], 0)
+        ts(T.f320[:], T.pb[:, 0:C], 0.0, OP.is_lt, [], ["f320", ("pb", 0)], float(C), OP.mult)
+        copy("S", T.ssb[:], T.pb[:, 0:C], [], ["ssb", ("pb", 0)])
+        take(ao, "sc0")
+        if r == 0:
+            unit(1)
+        send(partner, T[aa][:], T[ao][:], "arA%d" % r, ao)
+        tt(T.wa[:, 0:C], ind("f320", ao), T.aw[:], OP.add, ["f320", ao, "aw"], ["wa"])
+        scan("sc0", "wa")
+        take("wu", "sc0")
+        if r == 0:
+            unit(2)
+            unit(3)
+        for b in range(4):
+            mm(("pa", b), "ec", "es", tc, tsn, [("ec", b), tc, tsn], 128 * b)
+        for b in range(4):
+            mm(("pb", b), "ec", "es", ac, asn, [("ec", b), ac, asn], 128 * b)
+
+        def half(b):
+            copy("S", T.fh[:, C * b:C * b + C], T.pb[:, 512 * b:512 * b + C], [], [("fh", b), ("pb", b)], 0.5)
+
+        def ahead(b):
+            copy("S", T.fa[:, C * b:C * b + C], ind("fh", aa, C * b, C * b + C), [("fh", b), aa], [("fa", b)])
+
+        copy("S", T.wb[:, 0:C], ind("wa", "wu", 0, 2 * C), ["wa", "wu"], ["wb"])
+        ts(T.d1[:, 0:C], T.wa[:, 0:C], float(C), OP.is_lt, ["wa"], ["d1"], 1.0, OP.add)
+        scan("sc1", "f320")
+        ts(T.d2[:, 0:C], ind("d1", "wu", 0, 2 * C), 1.0, OP.add, ["d1", "wu"], ["d2"])
+        copy("S", T.wa[:, 0:C], ind("wb", "wu", 0, 2 * C), ["wb", "wu"], ["wa"])
+        scan("sc0", "wa")
+        take("wz", "sc0")
+        copy("S", T.smh[:], T.d2[:, 0:C], ["d2"], ["smh"])
+        ts(T.nf[:], ends("sc1"), T.qoff[:, 0:1], OP.subtract, ["sc1", "qoff"], ["nf"], 0.0, OP.is_equal)
+        src, oth, dcur, d_a, d_b = "wa", "wb", "d2", "d3", "d1"
+        lst, nxt = "wz", "wu"
+        for i, k in enumerate(STAGES[1:], 1):
+            copy("S", T[oth][:, 0:C], ind(src, lst, 0, 2 * C), [src, lst], [oth])
+            tt(T[d_a][:, 0:C], ind(dcur, lst, 0, 2 * C), T.smh[:], OP.add, [dcur, lst, "smh"], [d_a])
+            if i == 1:
+                tt(T.t4[:], T.nf[:], T.c640[:], OP.mult, ["nf", "c640"], ["t4"])
+            if k == 3:
+                copy("S", T[src][:, 0:C], ind(oth, lst, 0, 2 * C), [oth, lst], [src])
+                tt(T[d_b][:, 0:C], ind(d_a, lst, 0, 2 * C), T.smh[:], OP.add, [d_a, lst, "smh"], [d_b])
+                copy("S", T.smh[:], T[d_b][:, 0:C], [d_b], ["smh"])
+                scan("sc0", src)
+                if i == 1:
+                    ts(T.nfk[:], T.t4[:], T.qoff[:, 0:1], OP.add, ["t4", "qoff"], ["nfk"])
+                take(nxt, "sc0")
+                lst, nxt = nxt, lst
+                dcur, d_b = d_b, dcur
+            else:
+                src, dcur = oth, d_a
+        half(0)
+        half(1)
+        scan("sc0", src)
+        scan("sc1", dcur)
+        tt(T.t1[:], ends("sc0"), T.nfk[:], OP.max, ["sc0", "nfk"], ["t1"])
+        op("S", lambda e: e.activation(T.wf[:], ends("sc0"), AF.Identity, T.nqo[:, 0:1]), ["sc0", "nqo"], ["wf"])
+        op("S", lambda e: e.activation(T.wg[:], ends("sc0"), AF.Identity, T.nwg[:, 0:1], float(SLOPE)), ["sc0", "nwg"], ["wg"])
+        take("wu", "sc0")
+        ts(T.lu[:], T.t1[:], T.qoff[:, 0:1], OP.subtract, ["t1", "qoff"], ["lu"])
+        take("df", "sc1")
+        op("V", lambda e: e.tensor_copy(T.lw[:].indirect(T.lu[:, 0:K]), T[dcur][:, 0:C]), ["lu", dcur], ["lw"])
+        half(2)
+        half(3)
+        copy("S", T.lg[:], ind("lw", "wu", 0, 2 * C), ["lw", "wu"], ["lg"])
+        tt(T.t2[:], T.df[:], T.nf[:], OP.mult, ["df", "nf"], ["t2"])
+        tt(T.gg[:], T.wf[:], T.wg[:], OP.max, ["wf", "wg"], ["gg"])
+        tt(T.t3[:], T.gg[:], T.t2[:], OP.add, ["gg", "t2"], ["t3"])
+        tt(T.t5[:], T.gg[:], ends("sc1"), OP.subtract, ["gg", "sc1"], ["t5"])
+        copy("V", T.k1u[:], T.t3[:], ["t3"], ["k1u"])
+        op("V", lambda e: e.tensor_copy(T.tab[:].indirect(T.k1u[:, 0:K]), T.cb[:]), ["k1u", "cb"], ["tab"])
+        scan("sc2", "lg")
+        tt(T.t4[:], ends("sc2"), T.t5[:], OP.add, ["sc2", "t5"], ["t4"])
+        copy("V", T.k2u[:], T.t4[:], ["t4"], ["k2u"])
+        ts(T.mw[:], T.tab[:].indirect(T.k2u[:, 0:K]), 160.0, OP.add, ["tab", "k2u"], ["mw"])
+        for b in range(4):
+            ahead(b)
+        scan("sc0", "mw")
+        take(mo, "sc0")
+        send(partner, T[am][:], T[mo][:], "arM%d" % r, mo)
+        copy("V", T.sm[:], ind("ssb", mo), ["ssb", mo], ["sm"])
+        for b in (3, 2):
+            copy("S", T.fo[:, C * b:C * b + C], T.pa[:, 512 * b:512 * b + C], [], [("fo", b), ("pa", b)], 32.0)
+
+        def own(b):
+            copy("S", T.fm[:, C * (b - 2):C * (b - 1)], ind("fo", mo, C * b, C * b + C), [("fo", b), mo], [("fm", b)])
+
+        def early(b):
+            c = C * (b - 2)
+            tt(T.y3[:, c:c + C], T.pa[:, 512 * b:512 * b + C], T.fm[:, c:c + C], OP.add, [("fm", b)], [("y3", b), ("pa", b)])
+
+        def turn(b):
+            copy("S", T.xn[:, b:4 * C:4], ind("y3", mo, C * (b - 2), C * (b - 1)), [("y3", b), mo], [("xn", b)], 0.03125)
+
+        def scaled(b):
+            copy("S", T.rs[:, C * b:C * b + C], T.pa[:, 512 * b:512 * b + C], [], [("rs", b), ("pa", b)], 0.03125)
+
+        def late(b):
+            tt(T.xn[:, b:4 * C:4], ind("rs", mo, C * b, C * b + C), T.fo[:, C * b:C * b + C], OP.add, [("rs", b), mo, ("fo", b)], [("xn", b)])
+
+        copy("S", T.smh[:], ind("sm", "highu"), ["sm", "highu"], ["smh"])
+        if r == 0:
+            copy("V", T.cm[:, HALF:HALF + C], ind("mpi", "piu"), ["mpi", "piu"], ["cm"])
+            copy("S", T.qq[:, HALF:HALF + C], ind("qq", "mu16"), ["qq", "mu16"], [("qq", 1)])
+        if r == 2:
+            quant("vc", "vs", "vt")
+        tt(T.sw[:], ind("sm", "lowu"), T.smh[:], OP.is_gt, ["sm", "lowu", "smh"], ["sw"])
+        own(3)
+        scan("sc1", "sw")
+
+        def sigma():
+            tt(T.t2[:], ends("sc1"), T.chalf[:], OP.add, ["sc1", "chalf"], ["t2"])
+            ts(T.sgu[:], T.t2[:], float(HALF), OP.mult, ["t2", "nqh"], ["sgu"], T.nqh[:, 0:1], OP.add)
+
+        def through():
+            copy("S", T.qs[:], ind(qcur, "sgu", 0, HALF + C), [qcur, (qcur, 1), "sgu"], ["qs"])
+            copy("S", T.sgw[:], ind("cm", "sgu", 0, HALF + C), ["cm", "sgu"], ["sgw"])
+
+        if r < 2:
+            sigma()
+            through()
+            copy("S", T.lg[:], ind("qs", "pu"), ["qs", "pu"], ["lg"])
+        for b in range(4):
+            tt(T.zt[:, b:4 * C:4], ind("fh", am, C * b, C * b + C), T.fa[:, C * b:C * b + C], OP.add, [("fh", b), ("fa", b), am], [("zt", b)])
+        own(2)
+        for b in range(2):
+            copy("S", T.fo[:, C * b:C * b + C], T.pa[:, 512 * b:512 * b + C], [], [("fo", b), ("pa", b)])
+        quant(zc, zs, "zt", [("zt", b) for b in range(4)])
+        for b in (0, 2, 1, 3):
+            mm(("pa", b), "lc", "ls", zc, zs, ["lc", "ls", zc, zs], 128 * b)
+        if r < 2:
+            scan("sc2", "lg")
+            take("qpu", "sc2")
+        else:
+            sigma()
+        scaled(0)
+        early(2)
+        late(0)
+        scaled(1)
+        turn(2)
+        early(3)
+        late(1)
+        turn(3)
+        if r < 2:
+            copy("S", T.aw[:], ind("sgw", "qpu"), ["sgw", "qpu"], ["aw"])
+        else:
+            through()
+        quant("tc%d" % (r + 1), "ts%d" % (r + 1), "xn", [("xn", b) for b in range(4)])
+        if r < 2:
+            scan("sc1", "qs")
+            scan("sc0", "aw")
+        else:
+            scan("sc1", "qs")
+        take("qsu", "sc1")
+        copy("S", T[qnew][:, 0:C], ind("sgw", "qsu"), ["sgw", "qsu"], [qnew])
+        if r < 2:
+            copy("S", T[qnew][:, HALF:HALF + C], ind(qnew, "mu16"), [qnew, "mu16"], [(qnew, 1)])
+        else:
+            dma("S", [(T.qo[:], T[qnew][0:128:16, 0:C])], "stored", 16, [qnew], [])
+        qcur, qnew = qnew, qcur
+    dma("Y", [(T.oc[:], T.tc3[:].bitcast(dt.uint8))] + [(T.osc[4 * k:4 * k + 4, :], T.ts3[32 * k:32 * k + 4, :]) for k in range(4)], "stored", 96, ["tc3", "ts3"], [])
+    mm(("pb", 0), "vc", "vs", "tc3", "ts3", ["vc", "vs", "tc3", "ts3"], 0)
+    copy("V", T.sc2[:], T.pb[:, 0:C], [], ["sc2", ("pb", 0)])
+    dma("Y", [(T.y[:], T.sc2[:])], "stored", 112, ["sc2"], [])
+    g.sync.wait_ge(T.sem.stored, 112)
+    g.wait_ge(T.sem.sent, sent[0])
+    for q in ("V", "S", "T", "G"):
+        need("G", "q" + q, count[q])
+    for n, t in (("x", 16), ("u", 16), ("v", 16), ("wc", 16), ("ws", 16), ("pl", 16), ("ml", 16), ("qw", 256), ("mw", 256)):
+        need("G", "ld_" + n, t)

@@ -1,23 +1,21 @@
-from concourse.bass import DstId, RemoteDMATransfer
 from concourse.mybir import dt, AluOpType as OP, ActivationFunctionType as AF
 
 C = 320
 K = C // 16
+H = C // 2
 STEP = [1, 2, 4]
-STAGES = [3, 3, 3, 3, 2]
-BIG = 1024.0
-SLOPE, SHIFT = 164, -51997
-HALF = 512
-UNMET = 162
-NCELL = 53000
+STAGES = [2, 2, 2, 1, 1]
+ROW = 164
+MET = 4 * C
+BIG, BIG2 = 2.0 ** 19, 512.0
+SAME = C + ROW * C
+NCELL = SAME + C
+MODE = "LLEE"
+XORDER = [(0, 0), (0, 1), (1, 0), (0, 2), (1, 1), (0, 3), (1, 2), (1, 3)]
 
 
-def wide(*names):
-    return {n: ("sbuf", [128, C], "float32") for n in names}
-
-
-def double(*names):
-    return {n: ("sbuf", [128, 2 * C], "float32") for n in names}
+def wide(d, *names):
+    return {n: ("sbuf", [128, C], d) for n in names}
 
 
 def small(d, *names):
@@ -41,26 +39,29 @@ def codes(n, *pairs):
 
 
 SCRATCH = {
-    **tiles("x0", "xn", "zt", "fo", "fh", "fa"),
+    **tiles("x0", "xn", "zt", "fo", "fh", "fa", "fm", "y3"),
     "ut": ("sbuf", [128, 512], "bfloat16"), "vt": ("sbuf", [128, 512], "bfloat16"),
     **codes(128, ("uc", "us"), ("urc", "urs"), ("vc", "vs")), **codes(512, ("lc", "ls"), ("ec", "es")),
     **codes(C, *[("zc%d" % r, "zs%d" % r) for r in range(3)], *[("ac%d" % r, "as%d" % r) for r in range(3)], *[("tc%d" % r, "ts%d" % r) for r in range(4)]),
-    "eone": ("sbuf", [128, 516], "bfloat16"), "ebase": ("sbuf", [128, 516], "bfloat16"),
-    "qpi": ("sbuf", [128, C], "int32"), "mpi": ("sbuf", [128, C], "int32"), "ji": ("sbuf", [128, C], "int32"), "ja": ("sbuf", [128, C], "int32"),
-    "u8i": ("sbuf", [128, 8], "int32"), "upick": ("sbuf", [128, 8], "uint16"), "cb": ("sbuf", [128, C], "bfloat16"),
-    "fm": ("sbuf", [128, 2 * C], "bfloat16"), "y3": ("sbuf", [128, 2 * C], "bfloat16"),
-    **column("int32", "pi1", "pa1"), **column("float32", "pf1", "p20", "qoff", "nqo", "nwg", "nqh"),
-    **small("int32", "pli", "mli", "k16", "k1"),
-    **small("uint16", "pu", "mu16", "lowu", "highu", "piu", "ppu", "qpu", "wu", "wz", "lu", "k1u", "k2u", "sgu", "qsu"),
+    "ebase": ("sbuf", [128, 516], "bfloat16"),
+    "ji": ("sbuf", [128, 24], "int32"), "dg": ("sbuf", [128, 24], "float32"), "pat": ("sbuf", [128, 16], "float32"),
+    "u8i": ("sbuf", [128, 8], "int32"), "upick": ("sbuf", [128, 8], "uint16"),
+    **column("int32", "pi1", "pa1"), **column("float32", "qoff", "qoff2", "qz", "qy", "qk", "qm2", "tq"),
+    **small("int32", "pli", "qli", "mli", "k16"),
+    **small("uint16", "pu", "lowu", "highu", "qu", "lu", "k1u", "k2u", "sgu", "wz", "per"),
     **small("uint16", *["%s%d" % (n, r) for n in ("am", "aa", "mo", "ao") for r in range(3)]),
-    **small("float32", "coff", "c640", "chalf", "nf", "nfk", "wf", "wg", "gg", "df", "t1", "t2", "t3", "t4", "t5"),
-    **wide("md", "lg", "aw", "f320", "ssb", "sc0", "sc1", "sc2", "mw", "sm", "smh", "sw", "sgw", "qs"),
-    **double("wa", "wb", "d1", "d2", "d3"), **{n: ("sbuf", [128, HALF + C], "float32") for n in ("qq", "qr", "cm")},
-    "lw": ("sbuf", [128, 3 * C], "float32"), "tab": ("sbuf", [128, NCELL], "bfloat16"), "rs": ("sbuf", [128, 3 * C], "float32"),
+    **small("float32", "coff", "cc1", "cc2", "cc3", "ck", "dmu", "tgt", "nk", "fix", "wg", "t1", "t2", "t3", "t4", "t5"),
+    "tw": ("sbuf", [128, 3 * K], "float32"), "wu": ("sbuf", [128, 6 * K], "uint16"),
+    **wide("bfloat16", "fs", "cb", "mw", "sg", "sgw", "qs", "qn", "scf", "md", "md2"), **wide("float16", "sh0", "sh1"),
+    **wide("float32", "aw", "lg", "ssb", "sc0", "sc2", "sm", "sd"),
+    "wa": ("sbuf", [128, 4 * C], "float32"), "wb": ("sbuf", [128, 4 * C], "float32"),
+    "lw": ("sbuf", [128, MET + C], "float32"), "tab": ("sbuf", [128, NCELL], "bfloat16"),
+    "rs": ("sbuf", [128, 4 * C], "float32"),
     "pa": ("psum", [128, 2048], "float32"), "pb": ("psum", [128, 2048], "float32"),
 }
 
-SEMAPHORES = ["qV", "qS", "qT", "qG", "sent", "stored"] + ["ld_" + n for n in ("x", "u", "v", "wc", "ws", "pl", "ml", "qw", "mw")]
+LOADS = (("x", 16), ("u", 16), ("v", 16), ("wc", 16), ("ws", 16), ("pl", 16), ("ql", 16), ("ml", 16))
+SEMAPHORES = ["qV", "qS", "qT", "qG", "sent", "stored"] + ["ld_" + n for n, _ in LOADS]
 for _r in range(3):
     SEMAPHORES += ["arX%d" % _r, "arA%d" % _r, "arM%d" % _r]
 
@@ -147,14 +148,16 @@ def rank_program(g, core, T, topo):
         g.remote_dma(out, in_, T.sem[sem], T.sem.sent, pid, rid, topo.mask(core, dst))
         sent[0] += len(topo.engines(core, dst))
 
-    def copy(q, out, in_, reads, writes, scale=None):
-        if q == "S":
-            if scale is None:
-                op("S", lambda e: e.activation(out, in_, AF.Copy), reads, writes)
-            else:
-                op("S", lambda e: e.activation(out, in_, AF.Copy, 0.0, scale), reads, writes)
+    def act(out, in_, reads, writes, bias=None, scale=None):
+        if bias is not None:
+            op("S", lambda e: e.activation(out, in_, AF.Identity, bias, 1.0 if scale is None else scale), reads, writes)
+        elif scale is not None:
+            op("S", lambda e: e.activation(out, in_, AF.Copy, 0.0, scale), reads, writes)
         else:
-            op("V", lambda e: e.tensor_copy(out, in_), reads, writes)
+            op("S", lambda e: e.activation(out, in_, AF.Copy), reads, writes)
+
+    def copy(out, in_, reads, writes):
+        op("V", lambda e: e.tensor_copy(out, in_), reads, writes)
 
     def tt(out, a, b, o, reads, writes):
         op("V", lambda e: e.tensor_tensor(out, a, b, o), reads, writes)
@@ -165,24 +168,52 @@ def rank_program(g, core, T, topo):
         else:
             op("V", lambda e: e.tensor_scalar(out, a, s1, s2, o1, o2), reads, writes)
 
-    def fill(ap, value, key):
-        op("V", lambda e: e.memset(ap, value), [], [key])
+    def stt(out, a, b, o):
+        tt(T[out][:], T[a][:], T[b][:], o, [a, b], [out])
+
+    def sts(out, a, s1, o1, s2=None, o2=None):
+        cols = [s for s in (s1, s2) if isinstance(s, str)]
+        s1, s2 = [T[s][:, 0:1] if isinstance(s, str) else s for s in (s1, s2)]
+        ts(T[out][:], T[a][:], s1, o1, [a] + cols, [out], s2, o2)
+
+    def scopy(out, a):
+        copy(T[out][:], T[a][:], [a], [out])
 
     def ind(win, off, a=0, b=C):
         return T[win][:, a:b].indirect(T[off][:, 0:K])
 
-    def scan(dst, src):
-        op("V", lambda e: e.tensor_tensor_scan(T[dst][:], T.md[:], T[src][:, 0:C], 0.0, OP.add, OP.max), ["md", src], [dst])
+    def both(key):
+        return [(key, 0), (key, 1)]
+
+    def shared(out, o, win, a, b, off, c, bias, reads, key):
+        v, s = [T[win][:, a:b].indirect(T[off][:, c + i * K // 2:c + (i + 1) * K // 2]) for i in range(2)]
+        act(T[out][:, o + H:o + C], s, reads, [(key, 1)], bias)
+        if bias is None:
+            copy(T[out][:, o:o + H], v, reads, [(key, 0)])
+        else:
+            ts(T[out][:, o:o + H], v, bias, OP.add, reads, [(key, 0)])
+
+    def scan(dst, src, a, jump, reads):
+        op("V", lambda e: e.tensor_tensor_scan(T[dst][:], T[jump][:], T[src][:, a:a + C], 0.0, OP.add, OP.max), [jump] + reads, [dst])
 
     def ends(sc):
         return T[sc][:, 15:C:16]
 
-    def take(out, sc, extra=None, o=None):
-        ts(T[out][:], ends(sc), T.qoff[:, 0:1], OP.subtract, [sc, "qoff"], [out], extra, o)
+    def take(out, sc):
+        ts(T[out][:], ends(sc), T.qm2[:, 0:1], OP.subtract, [sc, "qm2"], [out])
+
+    def places(out, in_, less, reads, writes):
+        ts(out, in_, T[less][:, 0:1], OP.subtract, reads + [less], writes, 1.0 / ROW, OP.mult)
 
     def mm(bank, lc, ls, rc, rs, reads, a):
         buf, b = bank
         op("T", lambda e: e.matmul_mx(T[buf][:, 512 * b:512 * b + C], T[lc][:, a:a + 128], T[ls][:, a:a + 128], T[rc][:], T[rs][:], True, True), reads, [(buf, b)])
+
+    def bank(buf, b):
+        return T[buf][:, 512 * b:512 * b + C]
+
+    def block(buf, b):
+        return T[buf][:, C * b:C * b + C]
 
     def quant(c, s, t, keys=None):
         op("V", lambda e: e.quantize_mx(T[c][:], T[s][:], T[t][:]), keys or [t], [c, s])
@@ -192,13 +223,12 @@ def rank_program(g, core, T, topo):
 
     dma("S", [(T.ut[:], T.u[:])], "ld_u", 16, [], ["ut"])
     dma("S", [(T.x0[:], T.x[:])], "ld_x", 16, [], ["x0"])
-    dma("S", [(T.pli[:], T.pl[:])], "ld_pl", 16, [], ["pli"])
-    dma("S", [(T.mli[:], T.ml[:])], "ld_ml", 16, [], ["mli"])
-    dma("Y", [(T.qpi[i:128:16, :], T.ql[:]) for i in range(16)], "ld_qw", 256, [], ["qpi"])
+    dma("Y", [(T.qli[:], T.ql[:])], "ld_ql", 16, [], ["qli"])
+    dma("Y", [(T.pli[:], T.pl[:])], "ld_pl", 16, [], ["pli"])
     need("Y", "ld_x", 16)
+    dma("Y", [(T.mli[:], T.ml[:])], "ld_ml", 16, [], ["mli"])
     dma("Y", [(T.lc[:].bitcast(dt.uint8), T.wc[:])], "ld_wc", 16, [], ["lc"])
     dma("Y", [(T.ls[:], T.ws[:])], "ld_ws", 16, [], ["ls"])
-    dma("Y", [(T.mpi[i:128:16, :], T.ml[:]) for i in range(16)], "ld_mw", 256, [], ["mpi"])
     dma("Y", [(T.vt[:], T.v[:])], "ld_v", 16, [], ["vt"])
     for r in range(3):
         e = len(topo.engines(T.cores[rank ^ STEP[r]], core))
@@ -206,235 +236,236 @@ def rank_program(g, core, T, topo):
         arrives("arA%d" % r, e, ["aa%d" % r])
         arrives("arM%d" % r, e, ["am%d" % r])
 
-    def iota(name, a, b, step, base, mult, flag=False):
-        op("G", lambda e: e.iota(T[name][:, a:b], [[step, b - a]], base, mult, allow_small_or_imprecise_dtypes=True) if flag else e.iota(T[name][:, a:b], [[step, b - a]], base, mult), [], [name])
-    iota("pi1", 0, 1, 1, 0, 1)
-    iota("ji", 0, C, 1, 4096, -1)
-    iota("u8i", 0, 8, 16, 0, 0)
-    iota("k1", 0, K, 1, 0, 0)
-    iota("k16", 0, K, 16, 0, 0)
-    fill(T.eone[:], 1.0, "eone")
-    op("G", lambda e: e.affine_select(T.ebase[:], T.eone[:], [[-1, 516]], OP.is_equal, 0.0, 3, 4), ["eone"], ["ebase"])
-    iota("wa", C, 2 * C, 1, C, 0, True)
-    iota("wb", C, 2 * C, 1, C, 0, True)
-    iota("cb", 0, C, 1, -160, 0, True)
-    iota("cm", 0, C, 1, 0, 0, True)
-    ts(T.pa1[:], T.pi1[:], 15, OP.bitwise_and, ["pi1"], ["pa1"])
-    fill(T.d1[:, C:2 * C], 0.0, "d1")
-    ts(T.pf1[:], T.pa1[:], 1.0, OP.mult, ["pa1"], ["pf1"])
-    ts(T.ja[:], T.ji[:], 15, OP.bitwise_and, ["ji"], ["ja"])
-    ts(T.p20[:], T.pf1[:], 20.0, OP.mult, ["pf1"], ["p20"])
-    ts(T.qoff[:], T.pf1[:], -BIG, OP.mult, ["pf1"], ["qoff"], 15 * BIG, OP.add)
-    ts(T.nqo[:], T.pf1[:], BIG, OP.mult, ["pf1"], ["nqo"], -15 * BIG, OP.add)
-    ts(T.sc2[:], T.ja[:], 0.0, OP.is_equal, ["ja"], ["sc2"], -33 * BIG, OP.mult)
-    copy("V", T.upick[:], T.u8i[:], ["u8i"], ["upick"])
-    ts(T.piu[:], T.k1[:], T.p20[:, 0:1], OP.add, ["k1", "p20"], ["piu"])
-    ts(T.coff[:], T.k16[:], T.pf1[:, 0:1], OP.add, ["k16", "pf1"], ["coff"])
-    ts(T.md[:], T.sc2[:], BIG, OP.add, ["sc2"], ["md"])
-    ts(T.nwg[:], T.nqo[:], float(SLOPE), OP.mult, ["nqo"], ["nwg"], float(SHIFT), OP.add)
-    ts(T.c640[:], T.coff[:], float(2 * C), OP.add, ["coff"], ["c640"])
-    ts(T.chalf[:], T.coff[:], 1.0 / HALF, OP.mult, ["coff"], ["chalf"])
-    ts(T.nqh[:], T.nqo[:], float(HALF), OP.mult, ["nqo"], ["nqh"])
-    ts(T.k16[:], T.pli[:], 15, OP.bitwise_and, ["pli"], ["k16"])
-    ts(T.k1[:], T.pli[:], 4, OP.arith_shift_right, ["pli"], ["k1"])
-    copy("V", T.pu[:], T.pli[:], ["pli"], ["pu"])
-    ts(T.t1[:], T.k16[:], 20.0, OP.mult, ["k16"], ["t1"])
-    fill(T.lw[:, 0:C], float(2 * UNMET), "lw")
-    for n in ("d2", "d3"):
-        copy("S", T[n][:, C:2 * C], T.d1[:, C:2 * C], ["d1"], [n])
-
-    tt(T.t2[:], T.t1[:], T.k1[:], OP.add, ["t1", "k1"], ["t2"])
+    def iota(name, n, step, base, mult, flag=False):
+        op("G", lambda e: e.iota(T[name][:], [[step, n]], base, mult, allow_small_or_imprecise_dtypes=True) if flag else e.iota(T[name][:], [[step, n]], base, mult), [], [name])
+    iota("pi1", 1, 1, 0, 1)
+    iota("ji", 24, 1, 4095, -1)
+    iota("u8i", 8, 16, 0, 0)
+    iota("k16", K, 16, 0, 0)
+    iota("cb", C, 1, -H, 0, True)
+    op("V", lambda e: e.memset(T.ebase[:], 1.0), [], ["ebase"])
+    op("G", lambda e: e.affine_select(T.ebase[:], T.ebase[:], [[-1, 516]], OP.is_equal, 0.0, 3, 4), ["ebase"], ["ebase"])
+    sts("pa1", "pi1", 15, OP.bitwise_and)
+    sts("ji", "ji", 15, OP.bitwise_and)
+    scopy("tq", "pa1")
+    sts("qoff", "pa1", 15.0, OP.is_lt, BIG, OP.mult)
+    sts("dg", "ji", 0.0, OP.is_equal)
+    sts("qoff2", "pa1", 15.0, OP.is_lt, BIG2, OP.mult)
+    scopy("upick", "u8i")
+    ts(T.t1[:, 0:16], T.dg[:, 1:17], -3.0, OP.mult, ["dg"], ["t1"])
+    sts("per", "k16", 0.0, OP.mult, "tq", OP.add)
+    sts("coff", "k16", "tq", OP.add)
+    tt(T.pat[:], T.t1[:, 0:16], T.dg[:, 0:16], OP.add, ["t1", "dg"], ["pat"])
+    sts("qz", "qoff", ROW * H + 0.5, OP.subtract)
+    sts("qm2", "qoff2", float(H), OP.subtract)
+    sts("t2", "coff", float(ROW), OP.mult, "qoff", OP.add)
+    act(T.md[:], ind("pat", "per", 0, 16), ["pat", "per"], ["md"], scale=BIG)
+    act(T.md2[:], ind("pat", "per", 0, 16), ["pat", "per"], ["md2"], scale=BIG2)
+    sts("qy", "qoff", ROW * H - (H - 1) / 2, OP.subtract)
+    sts("qk", "qoff", float(ROW * (MET - H) - C), OP.add)
+    for j in (1, 2, 3):
+        sts("cc%d" % j, "t2", float(ROW * (j * C - H)), OP.add)
+    sts("ck", "coff", "qk", OP.add)
+    scopy("qu", "qli")
+    scopy("pu", "pli")
+    copy(T.qn[:].indirect(T.qu[:, 0:K]), T.cb[:], ["qu", "cb"], ["qn"])
     quant("uc", "us", "ut")
-    copy("V", T.ppu[:], T.t2[:], ["t2"], ["ppu"])
+    unit(0)
+    act(T.aw[:], ind("qn", "pu"), ["qn", "pu"], ["aw"], scale=float(ROW))
     op("S", lambda e: e.activation(T.urs[:], T.us[:].indirect(T.upick[:, 0:8]), AF.Copy), ["us", "upick"], ["urs"])
     op("V", lambda e: e.tensor_copy(T.urc[:].bitcast(dt.uint32), T.uc[:].bitcast(dt.uint32).indirect(T.upick[:, 0:8])), ["uc", "upick"], ["urc"])
-    copy("V", T.gg[:], T.mli[:], ["mli"], ["gg"])
-    copy("V", T.mu16[:], T.mli[:], ["mli"], ["mu16"])
-    tt(T.wf[:], T.gg[:], T.coff[:], OP.min, ["gg", "coff"], ["wf"])
-    tt(T.wg[:], T.gg[:], T.coff[:], OP.max, ["gg", "coff"], ["wg"])
+    unit(1)
+    unit(2)
     quant("tc0", "ts0", "x0")
-    copy("V", T.lowu[:], T.wf[:], ["wf"], ["lowu"])
-    copy("V", T.highu[:], T.wg[:], ["wg"], ["highu"])
-    copy("S", T.aw[:], ind("qpi", "ppu"), ["qpi", "ppu"], ["aw"])
-    copy("S", T.qq[:, 0:C], ind("qpi", "piu"), ["qpi", "piu"], ["qq"])
-    unit(0)
-    scan("sc0", "aw")
+    scan("sc2", "aw", 0, "md", ["aw"])
+    places(T.ao0[:], ends("sc2"), "qz", ["sc2"], ["ao0"])
 
-    qcur, qnew = "qq", "qr"
+    def mates():
+        return [lambda: stt("t1", "mli", "coff", OP.min),
+                lambda: stt("t2", "mli", "coff", OP.max),
+                lambda: stt("dmu", "mli", "coff", OP.subtract),
+                lambda: scopy("lowu", "t1"),
+                lambda: scopy("highu", "t2"),
+                lambda: sts("t3", "dmu", "qoff2", OP.mult),
+                lambda: stt("tgt", "coff", "t3", OP.subtract)]
+
     for r in range(3):
         partner = T.cores[rank ^ STEP[r]]
         tc, tsn, zc, zs = "tc%d" % r, "ts%d" % r, "zc%d" % r, "zs%d" % r
         ao, mo, aa, am, ac, asn = "ao%d" % r, "mo%d" % r, "aa%d" % r, "am%d" % r, "ac%d" % r, "as%d" % r
         send(partner, T[ac][:].bitcast(dt.uint8), T[tc][:].bitcast(dt.uint8), "arX%d" % r, tc)
         send(partner, T[asn][:], T[tsn][:], "arX%d" % r, tsn)
-        mm(("pb", 0), "urc", "urs", tc, tsn, ["urc", "urs", tc, tsn], 0)
-        ts(T.f320[:], T.pb[:, 0:C], 0.0, OP.is_lt, [], ["f320", ("pb", 0)], float(C), OP.mult)
-        copy("S", T.ssb[:], T.pb[:, 0:C], [], ["ssb", ("pb", 0)])
-        take(ao, "sc0")
-        if r == 0:
-            unit(1)
         send(partner, T[aa][:], T[ao][:], "arA%d" % r, ao)
-        tt(T.wa[:, 0:C], ind("f320", ao), T.aw[:], OP.add, ["f320", ao, "aw"], ["wa"])
-        scan("sc0", "wa")
-        take("wu", "sc0")
+        mm(("pb", 0), "urc", "urs", tc, tsn, ["urc", "urs", tc, tsn], 0)
+        ts(T.fs[:], bank("pb", 0), 0.0, OP.is_lt, [], ["fs", ("pb", 0)], float(ROW * MET), OP.mult)
+        act(T.ssb[:], bank("pb", 0), [], ["ssb", ("pb", 0)])
         if r == 0:
-            unit(2)
             unit(3)
-        for b in range(4):
-            mm(("pa", b), "ec", "es", tc, tsn, [("ec", b), tc, tsn], 128 * b)
-        for b in range(4):
-            mm(("pb", b), "ec", "es", ac, asn, [("ec", b), ac, asn], 128 * b)
+        tt(block("wa", 2), ind("fs", ao), T.aw[:], OP.add, ["fs", ao, "aw"], both(("wa", 2)))
+
+        def own(b, buf):
+            mm((buf, b), "ec", "es", tc, tsn, [("ec", b), tc, tsn], 128 * b)
 
         def half(b):
-            copy("S", T.fh[:, C * b:C * b + C], T.pb[:, 512 * b:512 * b + C], [], [("fh", b), ("pb", b)], 0.5)
+            act(block("fh", b), bank("pb", b), [], [("fh", b), ("pb", b)], scale=0.5)
+            if MODE[b] == "P":
+                own(b, "pb")
 
         def ahead(b):
-            copy("S", T.fa[:, C * b:C * b + C], ind("fh", aa, C * b, C * b + C), [("fh", b), aa], [("fa", b)])
+            act(block("fa", b), ind("fh", aa, C * b, C * b + C), [("fh", b), aa], [("fa", b)])
 
-        copy("S", T.wb[:, 0:C], ind("wa", "wu", 0, 2 * C), ["wa", "wu"], ["wb"])
-        ts(T.d1[:, 0:C], T.wa[:, 0:C], float(C), OP.is_lt, ["wa"], ["d1"], 1.0, OP.add)
-        scan("sc1", "f320")
-        ts(T.d2[:, 0:C], ind("d1", "wu", 0, 2 * C), 1.0, OP.add, ["d1", "wu"], ["d2"])
-        copy("S", T.wa[:, 0:C], ind("wb", "wu", 0, 2 * C), ["wb", "wu"], ["wa"])
-        scan("sc0", "wa")
-        take("wz", "sc0")
-        copy("S", T.smh[:], T.d2[:, 0:C], ["d2"], ["smh"])
-        ts(T.nf[:], ends("sc1"), T.qoff[:, 0:1], OP.subtract, ["sc1", "qoff"], ["nf"], 0.0, OP.is_equal)
-        src, oth, dcur, d_a, d_b = "wa", "wb", "d2", "d3", "d1"
-        lst, nxt = "wz", "wu"
-        for i, k in enumerate(STAGES[1:], 1):
-            copy("S", T[oth][:, 0:C], ind(src, lst, 0, 2 * C), [src, lst], [oth])
-            tt(T[d_a][:, 0:C], ind(dcur, lst, 0, 2 * C), T.smh[:], OP.add, [dcur, lst, "smh"], [d_a])
-            if i == 1:
-                tt(T.t4[:], T.nf[:], T.c640[:], OP.mult, ["nf", "c640"], ["t4"])
-            if k == 3:
-                copy("S", T[src][:, 0:C], ind(oth, lst, 0, 2 * C), [oth, lst], [src])
-                tt(T[d_b][:, 0:C], ind(d_a, lst, 0, 2 * C), T.smh[:], OP.add, [d_a, lst, "smh"], [d_b])
-                copy("S", T.smh[:], T[d_b][:, 0:C], [d_b], ["smh"])
-                scan("sc0", src)
-                if i == 1:
-                    ts(T.nfk[:], T.t4[:], T.qoff[:, 0:1], OP.add, ["t4", "qoff"], ["nfk"])
-                take(nxt, "sc0")
-                lst, nxt = nxt, lst
-                dcur, d_b = d_b, dcur
-            else:
-                src, dcur = oth, d_a
-        half(0)
-        half(1)
-        scan("sc0", src)
-        scan("sc1", dcur)
-        tt(T.t1[:], ends("sc0"), T.nfk[:], OP.max, ["sc0", "nfk"], ["t1"])
-        op("S", lambda e: e.activation(T.wf[:], ends("sc0"), AF.Identity, T.nqo[:, 0:1]), ["sc0", "nqo"], ["wf"])
-        op("S", lambda e: e.activation(T.wg[:], ends("sc0"), AF.Identity, T.nwg[:, 0:1], float(SLOPE)), ["sc0", "nwg"], ["wg"])
-        take("wu", "sc0")
-        ts(T.lu[:], T.t1[:], T.qoff[:, 0:1], OP.subtract, ["t1", "qoff"], ["lu"])
-        take("df", "sc1")
-        op("V", lambda e: e.tensor_copy(T.lw[:].indirect(T.lu[:, 0:K]), T[dcur][:, 0:C]), ["lu", dcur], ["lw"])
-        half(2)
-        half(3)
-        copy("S", T.lg[:], ind("lw", "wu", 0, 2 * C), ["lw", "wu"], ["lg"])
-        tt(T.t2[:], T.df[:], T.nf[:], OP.mult, ["df", "nf"], ["t2"])
-        tt(T.gg[:], T.wf[:], T.wg[:], OP.max, ["wf", "wg"], ["gg"])
-        tt(T.t3[:], T.gg[:], T.t2[:], OP.add, ["gg", "t2"], ["t3"])
-        tt(T.t5[:], T.gg[:], ends("sc1"), OP.subtract, ["gg", "sc1"], ["t5"])
-        copy("V", T.k1u[:], T.t3[:], ["t3"], ["k1u"])
-        op("V", lambda e: e.tensor_copy(T.tab[:].indirect(T.k1u[:, 0:K]), T.cb[:]), ["k1u", "cb"], ["tab"])
-        scan("sc2", "lg")
-        tt(T.t4[:], ends("sc2"), T.t5[:], OP.add, ["sc2", "t5"], ["t4"])
-        copy("V", T.k2u[:], T.t4[:], ["t4"], ["k2u"])
-        ts(T.mw[:], T.tab[:].indirect(T.k2u[:, 0:K]), 160.0, OP.add, ["tab", "k2u"], ["mw"])
+        gaps = [lambda: scan("scf", "fs", 0, "md", ["fs"]),
+                lambda: ts(T.t4[:], ends("scf"), T.qoff[:, 0:1], OP.is_gt, ["scf", "qoff"], ["t4"], BIG, OP.mult),
+                lambda: ts(T.t5[:], ends("scf"), T.qoff[:, 0:1], OP.is_gt, ["scf", "qoff"], ["t5"], float(SAME), OP.mult),
+                lambda: stt("nk", "t4", "cc2", OP.add),
+                lambda: stt("fix", "t5", "coff", OP.add)]
+        if r > 0:
+            gaps += [lambda: scan("sh1", "qn", 0, "md2", ["qn"]), lambda: take("qu", "sh1")]
+        else:
+            gaps += mates()
+            act(T.tab[:, SAME:SAME + C], T.cb[:], ["cb"], ["same"])
+
+        def gap():
+            if gaps:
+                gaps.pop(0)()
+
+        def keep(b):
+            act(block("fo", b), bank("pa", b), [], [("fo", b), ("pa", b)], scale=32.0 if MODE[b] == "E" else None)
+
+        def slots(buf, a):
+            return [key for j in range(a, 4) for key in both((buf, j))]
+
         for b in range(4):
-            ahead(b)
-        scan("sc0", "mw")
-        take(mo, "sc0")
+            own(b, "pa")
+        for b in range(4):
+            mm(("pb", b), "ec", "es", ac, asn, [("ec", b), ac, asn], 128 * b)
+        src, at, s, before = "wa", 2, 1, 0
+        for i, k in enumerate(STAGES):
+            cur, w0 = ("wa", "wb")[i % 2], 3 * K * (i % 2)
+            act(block(cur, 3), block(src, at), both((src, at)), both((cur, 3)), -float(s))
+            scan("sc0", src, C * at, "md", both((src, at)))
+            if i == 0:
+                keep(0)
+                keep(1)
+            else:
+                c = 3 * K - w0 + K * (2 - at)
+                act(block(cur, 2), T[src][:, C * at:4 * C].indirect(T.wu[:, c:c + K]), slots(src, at) + [("wu", c)], both((cur, 2)), float(before))
+            gap()
+            n = k + 1 if i < len(STAGES) - 1 else k
+            for j in range(n):
+                tt(T.tw[:, K * j:K * j + K], ends("sc0"), T["cc%d" % (j + 1)][:], OP.min, ["sc0", "cc%d" % (j + 1)], [("tw", j)])
+            gap()
+            for j in range(n):
+                places(T.wu[:, w0 + K * j:w0 + K * j + K], T.tw[:, K * j:K * j + K], "qz", [("tw", j)], [("wu", w0 + K * j)])
+            for j in range(k):
+                shared(cur, C * (1 - j), cur, C * (2 - j), 4 * C, "wu", w0 + K * j, float(s), slots(cur, 2 - j) + [("wu", w0 + K * j)], (cur, 1 - j))
+                gap()
+            src, at, s, before = cur, 2 - k, (k + 1) * s + before, s
+        while gaps:
+            gap()
+        scan("sc0", src, C * at, "md", both((src, at)))
+        keep(2)
+        keep(3)
+        for b in range(4):
+            half(b)
+        tt(T.t1[:], ends("sc0"), T.nk[:], OP.min, ["sc0", "nk"], ["t1"])
+        tt(T.t3[:], ends("sc0"), T.ck[:], OP.max, ["sc0", "ck"], ["t3"])
+        places(T.wz[:], ends("sc0"), "qy", ["sc0"], ["wz"])
+        places(T.lu[:], T.t1[:], "qy", ["t1"], ["lu"])
+        sts("k1u", "t3", "qk", OP.subtract)
+        sts("wg", "wz", float(ROW), OP.mult, float(C - 1 - ROW * MET), OP.add)
+        copy(T.lw[:].indirect(T.lu[:, 0:K]), block(src, at), ["lu"] + both((src, at)), ["lw"])
+        act(T.lg[:], ind("lw", "wz", 0, MET + C), ["lw", "wz"], ["lg"])
+        stt("t4", "wg", "fix", OP.max)
+        copy(T.tab[:, 0:SAME].indirect(T.k1u[:, 0:K]), T.cb[:], ["k1u", "cb"], ["tab"])
+        tt(T.t5[:], T.t4[:], ends("sc0"), OP.subtract, ["t4", "sc0"], ["t5"])
+        ahead(0)
+        ahead(1)
+        scan("sc2", "lg", 0, "md", ["lg"])
+        tt(T.t4[:], ends("sc2"), T.t5[:], OP.add, ["sc2", "t5"], ["t4"])
+        scopy("k2u", "t4")
+        shared("mw", 0, "tab", 0, NCELL, "k2u", 0, None, ["tab", "same", "k2u"], "mw")
+        ahead(2)
+        scan("sh0", "mw", 0, "md2", both("mw"))
+        take(mo, "sh0")
         send(partner, T[am][:], T[mo][:], "arM%d" % r, mo)
-        copy("V", T.sm[:], ind("ssb", mo), ["ssb", mo], ["sm"])
-        for b in (3, 2):
-            copy("S", T.fo[:, C * b:C * b + C], T.pa[:, 512 * b:512 * b + C], [], [("fo", b), ("pa", b)], 32.0)
-
-        def own(b):
-            copy("S", T.fm[:, C * (b - 2):C * (b - 1)], ind("fo", mo, C * b, C * b + C), [("fo", b), mo], [("fm", b)])
-
-        def early(b):
-            c = C * (b - 2)
-            tt(T.y3[:, c:c + C], T.pa[:, 512 * b:512 * b + C], T.fm[:, c:c + C], OP.add, [("fm", b)], [("y3", b), ("pa", b)])
-
-        def turn(b):
-            copy("S", T.xn[:, b:4 * C:4], ind("y3", mo, C * (b - 2), C * (b - 1)), [("y3", b), mo], [("xn", b)], 0.03125)
-
-        def scaled(b):
-            copy("S", T.rs[:, C * b:C * b + C], T.pa[:, 512 * b:512 * b + C], [], [("rs", b), ("pa", b)], 0.03125)
-
-        def late(b):
-            tt(T.xn[:, b:4 * C:4], ind("rs", mo, C * b, C * b + C), T.fo[:, C * b:C * b + C], OP.add, [("rs", b), mo, ("fo", b)], [("xn", b)])
-
-        copy("S", T.smh[:], ind("sm", "highu"), ["sm", "highu"], ["smh"])
-        if r == 0:
-            copy("V", T.cm[:, HALF:HALF + C], ind("mpi", "piu"), ["mpi", "piu"], ["cm"])
-            copy("S", T.qq[:, HALF:HALF + C], ind("qq", "mu16"), ["qq", "mu16"], [("qq", 1)])
+        shared("sm", 0, "ssb", 0, C, mo, 0, None, ["ssb", mo], "sm")
+        shared("sd", 0, "sm", 0, C, "highu", 0, None, both("sm") + ["highu"], "sd")
+        ahead(3)
+        tt(T.sg[:], ind("sm", "lowu"), T.sd[:], OP.is_gt, both("sm") + both("sd") + ["lowu"], ["sg"])
         if r == 2:
             quant("vc", "vs", "vt")
-        tt(T.sw[:], ind("sm", "lowu"), T.smh[:], OP.is_gt, ["sm", "lowu", "smh"], ["sw"])
-        own(3)
-        scan("sc1", "sw")
+        scan("sh1", "sg", 0, "md2", ["sg"])
+        tt(T.t3[:], ends("sh1"), T.dmu[:], OP.mult, ["sh1", "dmu"], ["t3"])
 
-        def sigma():
-            tt(T.t2[:], ends("sc1"), T.chalf[:], OP.add, ["sc1", "chalf"], ["t2"])
-            ts(T.sgu[:], T.t2[:], float(HALF), OP.mult, ["t2", "nqh"], ["sgu"], T.nqh[:, 0:1], OP.add)
+        def travel(b):
+            tt(T.zt[:, b:4 * C:4], ind("fh", am, C * b, C * b + C), block("fa", b), OP.add, [("fh", b), ("fa", b), am], [("zt", b)])
 
-        def through():
-            copy("S", T.qs[:], ind(qcur, "sgu", 0, HALF + C), [qcur, (qcur, 1), "sgu"], ["qs"])
-            copy("S", T.sgw[:], ind("cm", "sgu", 0, HALF + C), ["cm", "sgu"], ["sgw"])
+        travel(0)
+        stt("t2", "t3", "tgt", OP.add)
+        travel(1)
+        scopy("sgu", "t2")
+        travel(2)
+        travel(3)
+        turns = [b for b in range(4) if MODE[b] == "E"]
 
+        def turn():
+            if turns:
+                b = turns.pop(0)
+                act(block("fm", b), ind("fo", mo, C * b, C * b + C), [("fo", b), mo], [("fm", b)])
+
+        while turns:
+            turn()
+        act(T.sgw[:], ind("cb", "sgu"), ["cb", "sgu"], ["sgw"])
+        act(T.qs[:], ind("sgw", "qu"), ["sgw", "qu"], ["qs"])
         if r < 2:
-            sigma()
-            through()
-            copy("S", T.lg[:], ind("qs", "pu"), ["qs", "pu"], ["lg"])
-        for b in range(4):
-            tt(T.zt[:, b:4 * C:4], ind("fh", am, C * b, C * b + C), T.fa[:, C * b:C * b + C], OP.add, [("fh", b), ("fa", b), am], [("zt", b)])
-        own(2)
-        for b in range(2):
-            copy("S", T.fo[:, C * b:C * b + C], T.pa[:, 512 * b:512 * b + C], [], [("fo", b), ("pa", b)])
+            act(T.qn[:], ind("qs", "sgu"), ["qs", "sgu"], ["qn"])
+        else:
+            act(T.lg[:], ind("qs", "sgu"), ["qs", "sgu"], ["lg"], float(H))
+            dma("Y", [(T.qo[:], T.lg[0:128:16, :])], "stored", 16, ["lg"], [])
         quant(zc, zs, "zt", [("zt", b) for b in range(4)])
-        for b in (0, 2, 1, 3):
+        order = sorted(range(4), key=lambda b: "PLE".index(MODE[b]))
+        order = [order[0], order[2], order[1], order[3]]
+        for b in order:
             mm(("pa", b), "lc", "ls", zc, zs, ["lc", "ls", zc, zs], 128 * b)
+
+        def first(b):
+            if MODE[b] == "E":
+                tt(block("y3", b), bank("pa", b), block("fm", b), OP.add, [("fm", b)], [("y3", b), ("pa", b)])
+            else:
+                act(block("rs", b), bank("pa", b), [], [("rs", b), ("pa", b)], scale=0.03125)
+
+        def second(b):
+            xn = T.xn[:, b:4 * C:4]
+            if MODE[b] == "E":
+                act(xn, ind("y3", mo, C * b, C * b + C), [("y3", b), mo], [("xn", b)], scale=0.03125)
+            elif MODE[b] == "L":
+                tt(xn, ind("rs", mo, C * b, C * b + C), block("fo", b), OP.add, [("rs", b), mo, ("fo", b)], [("xn", b)])
+            else:
+                act(block("rm", b), ind("rs", mo, C * b, C * b + C), [("rs", b), mo], [("rm", b)])
+
+        def third(b):
+            if MODE[b] == "P":
+                tt(T.xn[:, b:4 * C:4], bank("pb", b), block("rm", b), OP.add, [("rm", b)], [("xn", b), ("pb", b)])
+
+        for what, i in XORDER:
+            (first, second, third)[what](order[i])
         if r < 2:
-            scan("sc2", "lg")
-            take("qpu", "sc2")
-        else:
-            sigma()
-        scaled(0)
-        early(2)
-        late(0)
-        scaled(1)
-        turn(2)
-        early(3)
-        late(1)
-        turn(3)
-        if r < 2:
-            copy("S", T.aw[:], ind("sgw", "qpu"), ["sgw", "qpu"], ["aw"])
-        else:
-            through()
+            act(T.aw[:], ind("qn", "pu"), ["qn", "pu"], ["aw"], scale=float(ROW))
         quant("tc%d" % (r + 1), "ts%d" % (r + 1), "xn", [("xn", b) for b in range(4)])
         if r < 2:
-            scan("sc1", "qs")
-            scan("sc0", "aw")
-        else:
-            scan("sc1", "qs")
-        take("qsu", "sc1")
-        copy("S", T[qnew][:, 0:C], ind("sgw", "qsu"), ["sgw", "qsu"], [qnew])
-        if r < 2:
-            copy("S", T[qnew][:, HALF:HALF + C], ind(qnew, "mu16"), [qnew, "mu16"], [(qnew, 1)])
-        else:
-            dma("S", [(T.qo[:], T[qnew][0:128:16, 0:C])], "stored", 16, [qnew], [])
-        qcur, qnew = qnew, qcur
+            scan("sc2", "aw", 0, "md", ["aw"])
+            places(T["ao%d" % (r + 1)][:], ends("sc2"), "qz", ["sc2"], ["ao%d" % (r + 1)])
     dma("Y", [(T.oc[:], T.tc3[:].bitcast(dt.uint8))] + [(T.osc[4 * k:4 * k + 4, :], T.ts3[32 * k:32 * k + 4, :]) for k in range(4)], "stored", 96, ["tc3", "ts3"], [])
-    mm(("pb", 0), "vc", "vs", "tc3", "ts3", ["vc", "vs", "tc3", "ts3"], 0)
-    copy("V", T.sc2[:], T.pb[:, 0:C], [], ["sc2", ("pb", 0)])
-    dma("Y", [(T.y[:], T.sc2[:])], "stored", 112, ["sc2"], [])
-    g.sync.wait_ge(T.sem.stored, 112)
+    for i in range(2):
+        op("T", lambda e: e.matmul_mx(T.pb[:, 512 * i:512 * i + H], T.vc[:], T.vs[:], T.tc3[:, H * i:H * i + H], T.ts3[:, H * i:H * i + H], True, True), ["vc", "vs", "tc3", "ts3"], [("pb", i)])
+    act(T.sc2[:, 0:H], T.pb[:, 0:H], [], ["sc2", ("pb", 0)])
+    copy(T.sc0[:, 0:H], T.pb[:, 512:512 + H], [], ["sc0", ("pb", 1)])
+    dma("S", [(T.y[:, 0:H], T.sc2[:, 0:H])], "stored", 112, ["sc2"], [])
+    dma("Y", [(T.y[:, H:C], T.sc0[:, 0:H])], "stored", 128, ["sc0"], [])
+    g.sync.wait_ge(T.sem.stored, 128)
     g.wait_ge(T.sem.sent, sent[0])
     for q in ("V", "S", "T", "G"):
         need("G", "q" + q, count[q])
-    for n, t in (("x", 16), ("u", 16), ("v", 16), ("wc", 16), ("ws", 16), ("pl", 16), ("ml", 16), ("qw", 256), ("mw", 256)):
+    for n, t in LOADS:
         need("G", "ld_" + n, t)

@@ -4,14 +4,13 @@ C = 320
 K = C // 16
 H = C // 2
 STEP = [1, 2, 4]
-STAGES = [2, 2, 2, 1, 1]
-ROW = 164
-MET = 4 * C
-BIG, BIG2 = 2.0 ** 19, 512.0
-SAME = C + ROW * C
+STAGES = 6
+U = 1.0 / 256
+MET = 3 * C
+BIG, BIG2 = 2048.0, 512.0
+SAME = C + H * C
 NCELL = SAME + C
-MODE = "LLEE"
-XORDER = [(0, 0), (0, 1), (1, 0), (0, 2), (1, 1), (0, 3), (1, 2), (1, 3)]
+PARTS = [(0, 192), (192, C)]
 
 
 def wide(d, *names):
@@ -46,21 +45,21 @@ SCRATCH = {
     "ebase": ("sbuf", [128, 516], "bfloat16"),
     "ji": ("sbuf", [128, 24], "int32"), "dg": ("sbuf", [128, 24], "float32"), "pat": ("sbuf", [128, 16], "float32"),
     "u8i": ("sbuf", [128, 8], "int32"), "upick": ("sbuf", [128, 8], "uint16"),
-    **column("int32", "pi1", "pa1"), **column("float32", "qoff", "qoff2", "qz", "qy", "qk", "qm2", "tq"),
+    **column("int32", "pi1", "pa1"), **column("float32", "qoff", "qoff2", "qz", "qm2", "tq"),
     **small("int32", "pli", "qli", "mli", "k16"),
     **small("uint16", "pu", "lowu", "highu", "qu", "lu", "k1u", "k2u", "sgu", "wz", "per"),
     **small("uint16", *["%s%d" % (n, r) for n in ("am", "aa", "mo", "ao") for r in range(3)]),
-    **small("float32", "coff", "cc1", "cc2", "cc3", "ck", "dmu", "tgt", "nk", "fix", "wg", "t1", "t2", "t3", "t4", "t5"),
-    "tw": ("sbuf", [128, 3 * K], "float32"), "wu": ("sbuf", [128, 6 * K], "uint16"),
-    **wide("bfloat16", "fs", "cb", "mw", "sg", "sgw", "qs", "qn", "scf", "md", "md2"), **wide("float16", "sh0", "sh1"),
+    **small("float32", "coff", "cc1", "cc2", "ck", "dmu", "tgt", "nk", "fix", "wg", "t1", "t2", "t3", "t4", "t5"),
+    "wu": ("sbuf", [128, 4 * K], "uint16"),
+    **wide("bfloat16", "fs", "cb", "mw", "sg", "sgw", "qs", "qn", "scf", "md", "md2", "md3"), **wide("float16", "sh0", "sh1"),
     **wide("float32", "aw", "lg", "ssb", "sc0", "sc2", "sm", "sd"),
-    "wa": ("sbuf", [128, 4 * C], "float32"), "wb": ("sbuf", [128, 4 * C], "float32"),
+    "wa": ("sbuf", [128, 3 * C], "float32"), "wb": ("sbuf", [128, 3 * C], "float32"),
     "lw": ("sbuf", [128, MET + C], "float32"), "tab": ("sbuf", [128, NCELL], "bfloat16"),
     "rs": ("sbuf", [128, 4 * C], "float32"),
     "pa": ("psum", [128, 2048], "float32"), "pb": ("psum", [128, 2048], "float32"),
 }
 
-LOADS = (("x", 16), ("u", 16), ("v", 16), ("wc", 16), ("ws", 16), ("pl", 16), ("ql", 16), ("ml", 16))
+LOADS = (("x0", 16), ("x1", 16), ("u", 16), ("v", 16), ("wc", 16), ("ws", 16), ("pl", 16), ("ql", 16), ("ml", 16))
 SEMAPHORES = ["qV", "qS", "qT", "qG", "sent", "stored"] + ["ld_" + n for n, _ in LOADS]
 for _r in range(3):
     SEMAPHORES += ["arX%d" % _r, "arA%d" % _r, "arM%d" % _r]
@@ -142,8 +141,8 @@ def rank_program(g, core, T, topo):
     op, dma, arrives, waits, need, count = make_queues(g, T)
     sent = [0]
 
-    def send(dst, out, in_, sem, key):
-        waits("G", [key], [])
+    def send(dst, out, in_, sem, keys):
+        waits("G", keys, [])
         rid, pid, _ = topo.addr(dst)
         g.remote_dma(out, in_, T.sem[sem], T.sem.sent, pid, rid, topo.mask(core, dst))
         sent[0] += len(topo.engines(core, dst))
@@ -185,10 +184,12 @@ def rank_program(g, core, T, topo):
     def both(key):
         return [(key, 0), (key, 1)]
 
-    def shared(out, o, win, a, b, off, c, bias, reads, key):
+    def shared(out, o, win, a, b, off, c, bias, reads, key, scale=None):
         v, s = [T[win][:, a:b].indirect(T[off][:, c + i * K // 2:c + (i + 1) * K // 2]) for i in range(2)]
-        act(T[out][:, o + H:o + C], s, reads, [(key, 1)], bias)
-        if bias is None:
+        act(T[out][:, o + H:o + C], s, reads, [(key, 1)], bias if scale is None else bias * scale, scale)
+        if scale is not None:
+            ts(T[out][:, o:o + H], v, bias, OP.add, reads, [(key, 0)], scale, OP.mult)
+        elif bias is None:
             copy(T[out][:, o:o + H], v, reads, [(key, 0)])
         else:
             ts(T[out][:, o:o + H], v, bias, OP.add, reads, [(key, 0)])
@@ -202,30 +203,32 @@ def rank_program(g, core, T, topo):
     def take(out, sc):
         ts(T[out][:], ends(sc), T.qm2[:, 0:1], OP.subtract, [sc, "qm2"], [out])
 
-    def places(out, in_, less, reads, writes):
-        ts(out, in_, T[less][:, 0:1], OP.subtract, reads + [less], writes, 1.0 / ROW, OP.mult)
+    def mm(bank, lc, ls, rc, rs, reads, a, part=(0, C)):
+        (buf, b), (c0, c1) = bank, part
+        op("T", lambda e: e.matmul_mx(T[buf][:, 512 * b:512 * b + c1 - c0], T[lc][:, a:a + 128], T[ls][:, a:a + 128], T[rc][:, c0:c1], T[rs][:, c0:c1], True, True), reads, [(buf, b)])
 
-    def mm(bank, lc, ls, rc, rs, reads, a):
-        buf, b = bank
-        op("T", lambda e: e.matmul_mx(T[buf][:, 512 * b:512 * b + C], T[lc][:, a:a + 128], T[ls][:, a:a + 128], T[rc][:], T[rs][:], True, True), reads, [(buf, b)])
+    def bank(buf, b, part=(0, C)):
+        return T[buf][:, 512 * b:512 * b + part[1] - part[0]]
 
-    def bank(buf, b):
-        return T[buf][:, 512 * b:512 * b + C]
+    def block(buf, b, part=(0, C)):
+        return T[buf][:, C * b + part[0]:C * b + part[1]]
 
-    def block(buf, b):
-        return T[buf][:, C * b:C * b + C]
+    def quant(c, s, t):
+        op("V", lambda e: e.quantize_mx(T[c][:], T[s][:], T[t][:]), [t], [c, s])
 
-    def quant(c, s, t, keys=None):
-        op("V", lambda e: e.quantize_mx(T[c][:], T[s][:], T[t][:]), keys or [t], [c, s])
+    def quant_part(c, s, t, i, reads):
+        c0, c1 = PARTS[i]
+        op("V", lambda e: e.quantize_mx(T[c][:, c0:c1], T[s][:, c0:c1], T[t][:, 4 * c0:4 * c1]), reads, [(c, i)])
 
     def unit(b):
         op("V", lambda e: e.quantize_mx(T.ec[:, 128 * b:128 * b + 128], T.es[:, 128 * b:128 * b + 128], T.ebase[:, 3 - b:515 - b]), ["ebase"], [("ec", b)])
 
     dma("S", [(T.ut[:], T.u[:])], "ld_u", 16, [], ["ut"])
-    dma("S", [(T.x0[:], T.x[:])], "ld_x", 16, [], ["x0"])
+    for i, (c0, c1) in enumerate(PARTS):
+        dma("S", [(T.x0[:, 4 * c0:4 * c1], T.x[:, 4 * c0:4 * c1])], "ld_x%d" % i, 16, [], [("x0", i)])
     dma("Y", [(T.qli[:], T.ql[:])], "ld_ql", 16, [], ["qli"])
     dma("Y", [(T.pli[:], T.pl[:])], "ld_pl", 16, [], ["pli"])
-    need("Y", "ld_x", 16)
+    need("Y", "ld_x1", 16)
     dma("Y", [(T.mli[:], T.ml[:])], "ld_ml", 16, [], ["mli"])
     dma("Y", [(T.lc[:].bitcast(dt.uint8), T.wc[:])], "ld_wc", 16, [], ["lc"])
     dma("Y", [(T.ls[:], T.ws[:])], "ld_ws", 16, [], ["ls"])
@@ -256,29 +259,27 @@ def rank_program(g, core, T, topo):
     sts("per", "k16", 0.0, OP.mult, "tq", OP.add)
     sts("coff", "k16", "tq", OP.add)
     tt(T.pat[:], T.t1[:, 0:16], T.dg[:, 0:16], OP.add, ["t1", "dg"], ["pat"])
-    sts("qz", "qoff", ROW * H + 0.5, OP.subtract)
+    sts("qz", "qoff", -1.0, OP.mult, float(H), OP.add)
     sts("qm2", "qoff2", float(H), OP.subtract)
-    sts("t2", "coff", float(ROW), OP.mult, "qoff", OP.add)
     act(T.md[:], ind("pat", "per", 0, 16), ["pat", "per"], ["md"], scale=BIG)
-    act(T.md2[:], ind("pat", "per", 0, 16), ["pat", "per"], ["md2"], scale=BIG2)
-    sts("qy", "qoff", ROW * H - (H - 1) / 2, OP.subtract)
-    sts("qk", "qoff", float(ROW * (MET - H) - C), OP.add)
-    for j in (1, 2, 3):
-        sts("cc%d" % j, "t2", float(ROW * (j * C - H)), OP.add)
-    sts("ck", "coff", "qk", OP.add)
+    for n, k in (("md2", BIG2 / BIG), ("md3", 1 / U)):
+        act(T[n][:], T.md[:], ["md"], [n], scale=k)
+    for j in (1, 2):
+        sts("cc%d" % j, "coff", float(j * C), OP.add)
+    sts("ck", "coff", float(2 * C), OP.add, 1 / U, OP.mult)
     scopy("qu", "qli")
     scopy("pu", "pli")
     copy(T.qn[:].indirect(T.qu[:, 0:K]), T.cb[:], ["qu", "cb"], ["qn"])
     quant("uc", "us", "ut")
     unit(0)
-    act(T.aw[:], ind("qn", "pu"), ["qn", "pu"], ["aw"], scale=float(ROW))
+    act(T.aw[:], ind("qn", "pu"), ["qn", "pu", "qz"], both("aw"), T.qz[:, 0:1])
     op("S", lambda e: e.activation(T.urs[:], T.us[:].indirect(T.upick[:, 0:8]), AF.Copy), ["us", "upick"], ["urs"])
     op("V", lambda e: e.tensor_copy(T.urc[:].bitcast(dt.uint32), T.uc[:].bitcast(dt.uint32).indirect(T.upick[:, 0:8])), ["uc", "upick"], ["urc"])
+    scan("sc2", "aw", 0, "md", both("aw"))
+    quant_part("tc0", "ts0", "x0", 0, [("x0", 0)])
+    copy(T.ao0[:], ends("sc2"), ["sc2"], ["ao0"])
+    quant_part("tc0", "ts0", "x0", 1, [("x0", 1)])
     unit(1)
-    unit(2)
-    quant("tc0", "ts0", "x0")
-    scan("sc2", "aw", 0, "md", ["aw"])
-    places(T.ao0[:], ends("sc2"), "qz", ["sc2"], ["ao0"])
 
     def mates():
         return [lambda: stt("t1", "mli", "coff", OP.min),
@@ -293,31 +294,31 @@ def rank_program(g, core, T, topo):
         partner = T.cores[rank ^ STEP[r]]
         tc, tsn, zc, zs = "tc%d" % r, "ts%d" % r, "zc%d" % r, "zs%d" % r
         ao, mo, aa, am, ac, asn = "ao%d" % r, "mo%d" % r, "aa%d" % r, "am%d" % r, "ac%d" % r, "as%d" % r
-        send(partner, T[ac][:].bitcast(dt.uint8), T[tc][:].bitcast(dt.uint8), "arX%d" % r, tc)
-        send(partner, T[asn][:], T[tsn][:], "arX%d" % r, tsn)
-        send(partner, T[aa][:], T[ao][:], "arA%d" % r, ao)
-        mm(("pb", 0), "urc", "urs", tc, tsn, ["urc", "urs", tc, tsn], 0)
-        ts(T.fs[:], bank("pb", 0), 0.0, OP.is_lt, [], ["fs", ("pb", 0)], float(ROW * MET), OP.mult)
-        act(T.ssb[:], bank("pb", 0), [], ["ssb", ("pb", 0)])
+        send(partner, T[ac][:].bitcast(dt.uint8), T[tc][:].bitcast(dt.uint8), "arX%d" % r, both(tc))
+        send(partner, T[asn][:], T[tsn][:], "arX%d" % r, both(tc))
+        for i, part in enumerate(PARTS):
+            mm(("pb", i), "urc", "urs", tc, tsn, ["urc", "urs", (tc, i)], 0, part)
+            ts(block("fs", 0, part), bank("pb", i, part), 0.0, OP.is_lt, [], [("fs", i), ("pb", i)], float(MET), OP.mult)
+            act(block("ssb", 0, part), bank("pb", i, part), [], [("ssb", i), ("pb", i)])
+            if i == 0 and r > 0:
+                copy(T[ao][:], ends("sc2"), ["sc2"], [ao])
+        send(partner, T[aa][:], T[ao][:], "arA%d" % r, [ao])
+        if r == 0:
+            unit(2)
+        tt(block("wa", 1), ind("fs", ao), T.aw[:], OP.add, both("fs") + both("aw") + [ao], both(("wa", 1)))
         if r == 0:
             unit(3)
-        tt(block("wa", 2), ind("fs", ao), T.aw[:], OP.add, ["fs", ao, "aw"], both(("wa", 2)))
-
-        def own(b, buf):
-            mm((buf, b), "ec", "es", tc, tsn, [("ec", b), tc, tsn], 128 * b)
 
         def half(b):
             act(block("fh", b), bank("pb", b), [], [("fh", b), ("pb", b)], scale=0.5)
-            if MODE[b] == "P":
-                own(b, "pb")
 
         def ahead(b):
             act(block("fa", b), ind("fh", aa, C * b, C * b + C), [("fh", b), aa], [("fa", b)])
 
-        gaps = [lambda: scan("scf", "fs", 0, "md", ["fs"]),
-                lambda: ts(T.t4[:], ends("scf"), T.qoff[:, 0:1], OP.is_gt, ["scf", "qoff"], ["t4"], BIG, OP.mult),
+        gaps = [lambda: scan("scf", "fs", 0, "md", both("fs")),
+                lambda: ts(T.t4[:], ends("scf"), T.qoff[:, 0:1], OP.is_gt, ["scf", "qoff"], ["t4"], BIG / U, OP.mult),
                 lambda: ts(T.t5[:], ends("scf"), T.qoff[:, 0:1], OP.is_gt, ["scf", "qoff"], ["t5"], float(SAME), OP.mult),
-                lambda: stt("nk", "t4", "cc2", OP.add),
+                lambda: stt("nk", "t4", "ck", OP.add),
                 lambda: stt("fix", "t5", "coff", OP.add)]
         if r > 0:
             gaps += [lambda: scan("sh1", "qn", 0, "md2", ["qn"]), lambda: take("qu", "sh1")]
@@ -330,140 +331,153 @@ def rank_program(g, core, T, topo):
                 gaps.pop(0)()
 
         def keep(b):
-            act(block("fo", b), bank("pa", b), [], [("fo", b), ("pa", b)], scale=32.0 if MODE[b] == "E" else None)
+            act(block("fo", b), bank("pa", b), [], [("fo", b), ("pa", b)], scale=32.0 if b >= 2 else None)
 
         def slots(buf, a):
-            return [key for j in range(a, 4) for key in both((buf, j))]
+            return [key for j in range(a, 3) for key in both((buf, j))]
 
         for b in range(4):
-            own(b, "pa")
+            mm(("pa", b), "ec", "es", tc, tsn, [("ec", b)] + both(tc), 128 * b)
         for b in range(4):
             mm(("pb", b), "ec", "es", ac, asn, [("ec", b), ac, asn], 128 * b)
-        src, at, s, before = "wa", 2, 1, 0
-        for i, k in enumerate(STAGES):
-            cur, w0 = ("wa", "wb")[i % 2], 3 * K * (i % 2)
-            act(block(cur, 3), block(src, at), both((src, at)), both((cur, 3)), -float(s))
+        keep(0)
+        keep(1)
+        src, at, s, before = "wa", 1, 1, 0
+        for i in range(STAGES):
+            cur, w0, last = ("wa", "wb")[i % 2], 2 * K * (i % 2), i == STAGES - 1
             scan("sc0", src, C * at, "md", both((src, at)))
             if i == 0:
-                keep(0)
-                keep(1)
-            else:
-                c = 3 * K - w0 + K * (2 - at)
-                act(block(cur, 2), T[src][:, C * at:4 * C].indirect(T.wu[:, c:c + K]), slots(src, at) + [("wu", c)], both((cur, 2)), float(before))
-            gap()
-            n = k + 1 if i < len(STAGES) - 1 else k
-            for j in range(n):
-                tt(T.tw[:, K * j:K * j + K], ends("sc0"), T["cc%d" % (j + 1)][:], OP.min, ["sc0", "cc%d" % (j + 1)], [("tw", j)])
-            gap()
-            for j in range(n):
-                places(T.wu[:, w0 + K * j:w0 + K * j + K], T.tw[:, K * j:K * j + K], "qz", [("tw", j)], [("wu", w0 + K * j)])
-            for j in range(k):
-                shared(cur, C * (1 - j), cur, C * (2 - j), 4 * C, "wu", w0 + K * j, float(s), slots(cur, 2 - j) + [("wu", w0 + K * j)], (cur, 1 - j))
+                act(block(cur, 2), block(src, at), both((src, at)), both((cur, 2)), -s * U)
+                keep(2)
                 gap()
-            src, at, s, before = cur, 2 - k, (k + 1) * s + before, s
+            else:
+                c = 3 * K - w0
+                act(block(cur, 1), T[src][:].indirect(T.wu[:, c:c + K]), slots(src, 0) + [("wu", c)], both((cur, 1)), before * U)
+                ts(block(cur, 2, (0, 256)), block(src, at, (0, 256)), -s * U, OP.add, both((src, at)), [((cur, 2), 0)])
+                act(block(cur, 2, (256, C)), block(src, at, (256, C)), both((src, at)), [((cur, 2), 1)], -s * U)
+            for j in range(1 if last else 2):
+                tt(T.wu[:, w0 + K * j:w0 + K * j + K], ends("sc0"), T["cc%d" % (j + 1)][:], OP.min, ["sc0", "cc%d" % (j + 1)], [("wu", w0 + K * j)])
+            gap()
+            shared(cur, 0, cur, C, 3 * C, "wu", w0, s * U, slots(cur, 1) + [("wu", w0)], (cur, 0), 1 / U if last else None)
+            gap()
+            src, at, s, before = cur, 0, 2 * s + before, s
         while gaps:
             gap()
-        scan("sc0", src, C * at, "md", both((src, at)))
-        keep(2)
+        scan("sc0", src, 0, "md3", both((src, 0)))
         keep(3)
         for b in range(4):
             half(b)
         tt(T.t1[:], ends("sc0"), T.nk[:], OP.min, ["sc0", "nk"], ["t1"])
-        tt(T.t3[:], ends("sc0"), T.ck[:], OP.max, ["sc0", "ck"], ["t3"])
-        places(T.wz[:], ends("sc0"), "qy", ["sc0"], ["wz"])
-        places(T.lu[:], T.t1[:], "qy", ["t1"], ["lu"])
-        sts("k1u", "t3", "qk", OP.subtract)
-        sts("wg", "wz", float(ROW), OP.mult, float(C - 1 - ROW * MET), OP.add)
-        copy(T.lw[:].indirect(T.lu[:, 0:K]), block(src, at), ["lu"] + both((src, at)), ["lw"])
+        ts(T.wz[:], ends("sc0"), (H - 1) / 2, OP.subtract, ["sc0"], ["wz"], U, OP.mult)
+        sts("lu", "t1", (H - 1) / 2, OP.subtract, U, OP.mult)
+        sts("t3", "wz", H - 1 / U, OP.mult, float(C - H * MET), OP.add)
+        sts("wg", "wz", float(H), OP.mult, float(C - 1 - H * MET), OP.add)
+        tt(T.t2[:], ends("sc0"), T.t3[:], OP.add, ["sc0", "t3"], ["t2"])
+        copy(T.lw[:].indirect(T.lu[:, 0:K]), block(src, 0), ["lu"] + both((src, 0)), ["lw"])
+        ahead(0)
         act(T.lg[:], ind("lw", "wz", 0, MET + C), ["lw", "wz"], ["lg"])
+        stt("k1u", "t2", "coff", OP.max)
         stt("t4", "wg", "fix", OP.max)
         copy(T.tab[:, 0:SAME].indirect(T.k1u[:, 0:K]), T.cb[:], ["k1u", "cb"], ["tab"])
         tt(T.t5[:], T.t4[:], ends("sc0"), OP.subtract, ["t4", "sc0"], ["t5"])
-        ahead(0)
         ahead(1)
-        scan("sc2", "lg", 0, "md", ["lg"])
-        tt(T.t4[:], ends("sc2"), T.t5[:], OP.add, ["sc2", "t5"], ["t4"])
-        scopy("k2u", "t4")
-        shared("mw", 0, "tab", 0, NCELL, "k2u", 0, None, ["tab", "same", "k2u"], "mw")
         ahead(2)
+        scan("sc2", "lg", 0, "md3", ["lg"])
+        tt(T.k2u[:], ends("sc2"), T.t5[:], OP.add, ["sc2", "t5"], ["k2u"])
+        shared("mw", 0, "tab", 0, NCELL, "k2u", 0, None, ["tab", "same", "k2u"], "mw")
+        ahead(3)
         scan("sh0", "mw", 0, "md2", both("mw"))
         take(mo, "sh0")
-        send(partner, T[am][:], T[mo][:], "arM%d" % r, mo)
-        shared("sm", 0, "ssb", 0, C, mo, 0, None, ["ssb", mo], "sm")
+        send(partner, T[am][:], T[mo][:], "arM%d" % r, [mo])
+        shared("sm", 0, "ssb", 0, C, mo, 0, None, both("ssb") + [mo], "sm")
         shared("sd", 0, "sm", 0, C, "highu", 0, None, both("sm") + ["highu"], "sd")
-        ahead(3)
         tt(T.sg[:], ind("sm", "lowu"), T.sd[:], OP.is_gt, both("sm") + both("sd") + ["lowu"], ["sg"])
         if r == 2:
             quant("vc", "vs", "vt")
         scan("sh1", "sg", 0, "md2", ["sg"])
         tt(T.t3[:], ends("sh1"), T.dmu[:], OP.mult, ["sh1", "dmu"], ["t3"])
 
-        def travel(b):
-            tt(T.zt[:, b:4 * C:4], ind("fh", am, C * b, C * b + C), block("fa", b), OP.add, [("fh", b), ("fa", b), am], [("zt", b)])
+        def travel(b, i):
+            c0, c1 = PARTS[i]
+            tt(T.zt[:, 4 * c0 + b:4 * c1:4], block("fh", b).indirect(T[am][:, c0 // 16:c1 // 16]), block("fa", b, PARTS[i]), OP.add, [("fh", b), ("fa", b), am], [("zt", b, i)])
 
-        travel(0)
-        stt("t2", "t3", "tgt", OP.add)
-        travel(1)
-        scopy("sgu", "t2")
-        travel(2)
-        travel(3)
-        turns = [b for b in range(4) if MODE[b] == "E"]
+        def layer(i, order):
+            quant_part(zc, zs, "zt", i, [("zt", b, i) for b in range(4)])
+            for b in order:
+                mm((("pa", "pb")[i], b), "lc", "ls", zc, zs, ["lc", "ls", (zc, i)], 128 * b, PARTS[i])
 
-        def turn():
-            if turns:
-                b = turns.pop(0)
-                act(block("fm", b), ind("fo", mo, C * b, C * b + C), [("fo", b), mo], [("fm", b)])
+        def early(b, i):
+            buf = ("pa", "pb")[i]
+            tt(block("y3", b, PARTS[i]), bank(buf, b, PARTS[i]), block("fm", b, PARTS[i]), OP.add, [("fm", b)], [(("y3", b), i), (buf, b)])
 
-        while turns:
-            turn()
+        def scaled(b, i):
+            buf = ("pa", "pb")[i]
+            act(block("rs", b, PARTS[i]), bank(buf, b, PARTS[i]), [], [(("rs", b), i), (buf, b)], scale=0.03125)
+
+        def turn(b, part, keys):
+            c0, c1 = part
+            act(T.xn[:, 4 * c0 + b:4 * c1:4], block("y3", b).indirect(T[mo][:, c0 // 16:c1 // 16]), both(("y3", b)) + [mo], keys, scale=0.03125)
+
+        def late(b, part, keys):
+            c0, c1 = part
+            tt(T.xn[:, 4 * c0 + b:4 * c1:4], block("rs", b).indirect(T[mo][:, c0 // 16:c1 // 16]), block("fo", b, part), OP.add, both(("rs", b)) + [mo, ("fo", b)], keys)
+
+        def state(i):
+            quant_part("tc%d" % (r + 1), "ts%d" % (r + 1), "xn", i, [(("xn", b), i) for b in range(4)])
+
+        for b in (2, 3):
+            act(block("fm", b), ind("fo", mo, C * b, C * b + C), [("fo", b), mo], [("fm", b)])
+        travel(0, 0)
+        stt("sgu", "t3", "tgt", OP.add)
+        travel(1, 0)
         act(T.sgw[:], ind("cb", "sgu"), ["cb", "sgu"], ["sgw"])
         act(T.qs[:], ind("sgw", "qu"), ["sgw", "qu"], ["qs"])
+        travel(2, 0)
+        travel(3, 0)
+        travel(0, 1)
+        layer(0, (2, 3, 0, 1))
+        for b in (1, 2, 3):
+            travel(b, 1)
         if r < 2:
             act(T.qn[:], ind("qs", "sgu"), ["qs", "sgu"], ["qn"])
         else:
             act(T.lg[:], ind("qs", "sgu"), ["qs", "sgu"], ["lg"], float(H))
             dma("Y", [(T.qo[:], T.lg[0:128:16, :])], "stored", 16, ["lg"], [])
-        quant(zc, zs, "zt", [("zt", b) for b in range(4)])
-        order = sorted(range(4), key=lambda b: "PLE".index(MODE[b]))
-        order = [order[0], order[2], order[1], order[3]]
-        for b in order:
-            mm(("pa", b), "lc", "ls", zc, zs, ["lc", "ls", zc, zs], 128 * b)
-
-        def first(b):
-            if MODE[b] == "E":
-                tt(block("y3", b), bank("pa", b), block("fm", b), OP.add, [("fm", b)], [("y3", b), ("pa", b)])
-            else:
-                act(block("rs", b), bank("pa", b), [], [("rs", b), ("pa", b)], scale=0.03125)
-
-        def second(b):
-            xn = T.xn[:, b:4 * C:4]
-            if MODE[b] == "E":
-                act(xn, ind("y3", mo, C * b, C * b + C), [("y3", b), mo], [("xn", b)], scale=0.03125)
-            elif MODE[b] == "L":
-                tt(xn, ind("rs", mo, C * b, C * b + C), block("fo", b), OP.add, [("rs", b), mo, ("fo", b)], [("xn", b)])
-            else:
-                act(block("rm", b), ind("rs", mo, C * b, C * b + C), [("rs", b), mo], [("rm", b)])
-
-        def third(b):
-            if MODE[b] == "P":
-                tt(T.xn[:, b:4 * C:4], bank("pb", b), block("rm", b), OP.add, [("rm", b)], [("xn", b), ("pb", b)])
-
-        for what, i in XORDER:
-            (first, second, third)[what](order[i])
+        scaled(0, 0)
+        scaled(1, 0)
+        early(2, 0)
+        layer(1, (2, 0, 3, 1))
+        early(3, 0)
         if r < 2:
-            act(T.aw[:], ind("qn", "pu"), ["qn", "pu"], ["aw"], scale=float(ROW))
-        quant("tc%d" % (r + 1), "ts%d" % (r + 1), "xn", [("xn", b) for b in range(4)])
+            shared("aw", 0, "qn", 0, C, "pu", 0, T.qz[:, 0:1], ["qn", "pu"], "aw")
+        early(2, 1)
+        scaled(0, 1)
+        early(3, 1)
+        scaled(1, 1)
         if r < 2:
-            scan("sc2", "aw", 0, "md", ["aw"])
-            places(T["ao%d" % (r + 1)][:], ends("sc2"), "qz", ["sc2"], ["ao%d" % (r + 1)])
-    dma("Y", [(T.oc[:], T.tc3[:].bitcast(dt.uint8))] + [(T.osc[4 * k:4 * k + 4, :], T.ts3[32 * k:32 * k + 4, :]) for k in range(4)], "stored", 96, ["tc3", "ts3"], [])
-    for i in range(2):
-        op("T", lambda e: e.matmul_mx(T.pb[:, 512 * i:512 * i + H], T.vc[:], T.vs[:], T.tc3[:, H * i:H * i + H], T.ts3[:, H * i:H * i + H], True, True), ["vc", "vs", "tc3", "ts3"], [("pb", i)])
-    act(T.sc2[:, 0:H], T.pb[:, 0:H], [], ["sc2", ("pb", 0)])
-    copy(T.sc0[:, 0:H], T.pb[:, 512:512 + H], [], ["sc0", ("pb", 1)])
-    dma("S", [(T.y[:, 0:H], T.sc2[:, 0:H])], "stored", 112, ["sc2"], [])
-    dma("Y", [(T.y[:, H:C], T.sc0[:, 0:H])], "stored", 128, ["sc0"], [])
-    g.sync.wait_ge(T.sem.stored, 128)
+            for b in range(2):
+                turn(2 + b, (0, C), both(("xn", 2 + b)))
+                late(b, (0, C), both(("xn", b)))
+            state(0)
+            state(1)
+            scan("sc2", "aw", 0, "md", both("aw"))
+        else:
+            for i, part in enumerate(PARTS):
+                for b in range(2):
+                    turn(2 + b, part, [(("xn", 2 + b), i)])
+                    late(b, part, [(("xn", b), i)])
+                    if (i, b) == (1, 0):
+                        state(0)
+            state(1)
+    for i, (c0, c1) in enumerate(PARTS):
+        mm(("pb", i), "vc", "vs", "tc3", "ts3", ["vc", "vs", ("tc3", i)], 0, PARTS[i])
+        dma("Y", [(T.oc[:, 4 * c0:4 * c1], T.tc3[:, c0:c1].bitcast(dt.uint8))], "stored", 32 + 16 * i, [("tc3", i)], [])
+    act(block("sc0", 0, PARTS[0]), bank("pb", 0, PARTS[0]), [], ["sc0", ("pb", 0)])
+    dma("S", [(block("y", 0, PARTS[0]), block("sc0", 0, PARTS[0]))], "stored", 64, ["sc0"], [])
+    copy(block("sc2", 0, PARTS[1]), bank("pb", 1, PARTS[1]), [], ["sc2", ("pb", 1)])
+    dma("Y", [(T.osc[4 * k:4 * k + 4, :], T.ts3[32 * k:32 * k + 4, :]) for k in range(4)], "stored", 128, both("tc3"), [])
+    dma("S", [(block("y", 0, PARTS[1]), block("sc2", 0, PARTS[1]))], "stored", 144, ["sc2"], [])
+    g.sync.wait_ge(T.sem.stored, 144)
     g.wait_ge(T.sem.sent, sent[0])
     for q in ("V", "S", "T", "G"):
         need("G", "q" + q, count[q])

@@ -5,10 +5,14 @@ K = C // 16
 H = C // 2
 STEP = [1, 2, 4]
 STAGES = 6
-U = 1.0 / 256
+ROW = 164
+U = 1.0 / ROW
+LEAD, MID = -59, (H - 1) / 2
 MET = 3 * C
 BIG, BIG2 = 2048.0, 512.0
-SAME = C + H * C
+ROUND = 1.5 * 2 ** 23
+CELL0 = ROW * MET - MID - C
+SAME = C + ROW * C
 NCELL = SAME + C
 PARTS = [(0, 192), (192, C)]
 
@@ -48,12 +52,13 @@ SCRATCH = {
     **column("int32", "pi1", "pa1"), **column("float32", "qoff", "qoff2", "qz", "qm2", "tq"),
     **small("int32", "pli", "qli", "mli", "k16"),
     **small("uint16", "pu", "lowu", "highu", "qu", "lu", "k1u", "k2u", "sgu", "wz", "per"),
-    **small("uint16", *["%s%d" % (n, r) for n in ("am", "aa", "mo", "ao") for r in range(3)]),
+    **small("uint16", *["%s%d" % (n, r) for n in ("aa", "mo", "ao") for r in range(3)]),
+    **{"am%d" % r: ("sbuf", [128, K + 4], "uint16") for r in range(3)},
     **small("float32", "coff", "cc1", "cc2", "ck", "dmu", "tgt", "nk", "fix", "wg", "t1", "t2", "t3", "t4", "t5"),
     "wu": ("sbuf", [128, 4 * K], "uint16"),
     **wide("bfloat16", "fs", "cb", "mw", "sg", "sgw", "qs", "qn", "scf", "md", "md2", "md3"), **wide("float16", "sh0", "sh1"),
     **wide("float32", "aw", "lg", "ssb", "sc0", "sc2", "sm", "sd"),
-    "wa": ("sbuf", [128, 3 * C], "float32"), "wb": ("sbuf", [128, 3 * C], "float32"),
+    "wa": ("sbuf", [128, (2 * STAGES + 1) * C], "float32"),
     "lw": ("sbuf", [128, MET + C], "float32"), "tab": ("sbuf", [128, NCELL], "bfloat16"),
     "rs": ("sbuf", [128, 4 * C], "float32"),
     "pa": ("psum", [128, 2048], "float32"), "pb": ("psum", [128, 2048], "float32"),
@@ -62,7 +67,7 @@ SCRATCH = {
 LOADS = (("x0", 16), ("x1", 16), ("u", 16), ("v", 16), ("wc", 16), ("ws", 16), ("pl", 16), ("ql", 16), ("ml", 16))
 SEMAPHORES = ["qV", "qS", "qT", "qG", "sent", "stored"] + ["ld_" + n for n, _ in LOADS]
 for _r in range(3):
-    SEMAPHORES += ["arX%d" % _r, "arA%d" % _r, "arM%d" % _r]
+    SEMAPHORES += ["arX%d" % _r, "arA%d" % _r, "arM%d0" % _r, "arM%d1" % _r]
 
 
 def make_queues(g, T):
@@ -184,21 +189,23 @@ def rank_program(g, core, T, topo):
     def both(key):
         return [(key, 0), (key, 1)]
 
-    def shared(out, o, win, a, b, off, c, bias, reads, key, scale=None):
-        v, s = [T[win][:, a:b].indirect(T[off][:, c + i * K // 2:c + (i + 1) * K // 2]) for i in range(2)]
-        act(T[out][:, o + H:o + C], s, reads, [(key, 1)], bias if scale is None else bias * scale, scale)
-        if scale is not None:
-            ts(T[out][:, o:o + H], v, bias, OP.add, reads, [(key, 0)], scale, OP.mult)
-        elif bias is None:
-            copy(T[out][:, o:o + H], v, reads, [(key, 0)])
+    def shared(out, o, win, a, b, off, c, bias, reads, key, n=H):
+        v, s = [T[win][:, a:b].indirect(T[off][:, c + c0 // 16:c + c1 // 16]) for c0, c1 in ((0, n), (n, C))]
+        act(T[out][:, o + n:o + C], s, reads, [(key, 1)], bias)
+        if bias is None:
+            copy(T[out][:, o:o + n], v, reads, [(key, 0)])
         else:
-            ts(T[out][:, o:o + H], v, bias, OP.add, reads, [(key, 0)])
+            ts(T[out][:, o:o + n], v, bias, OP.add, reads, [(key, 0)])
 
-    def scan(dst, src, a, jump, reads):
-        op("V", lambda e: e.tensor_tensor_scan(T[dst][:], T[jump][:], T[src][:, a:a + C], 0.0, OP.add, OP.max), [jump] + reads, [dst])
+    def scan(dst, src, a, jump, reads, part=(0, C), keys=None):
+        c0, c1 = part
+        op("V", lambda e: e.tensor_tensor_scan(T[dst][:, c0:c1], T[jump][:, c0:c1], T[src][:, a + c0:a + c1], 0.0, OP.add, OP.max), [jump] + reads, keys or [dst])
 
-    def ends(sc):
-        return T[sc][:, 15:C:16]
+    def ends(sc, part=(0, C)):
+        return T[sc][:, part[0] + 15:part[1]:16]
+
+    def short(name, part, c=0):
+        return T[name][:, c + part[0] // 16:c + part[1] // 16]
 
     def take(out, sc):
         ts(T[out][:], ends(sc), T.qm2[:, 0:1], OP.subtract, [sc, "qm2"], [out])
@@ -237,7 +244,8 @@ def rank_program(g, core, T, topo):
         e = len(topo.engines(T.cores[rank ^ STEP[r]], core))
         arrives("arX%d" % r, 2 * e, ["ac%d" % r, "as%d" % r])
         arrives("arA%d" % r, e, ["aa%d" % r])
-        arrives("arM%d" % r, e, ["am%d" % r])
+        for i in range(2):
+            arrives("arM%d%d" % (r, i), e, [("am%d" % r, i)])
 
     def iota(name, n, step, base, mult, flag=False):
         op("G", lambda e: e.iota(T[name][:], [[step, n]], base, mult, allow_small_or_imprecise_dtypes=True) if flag else e.iota(T[name][:], [[step, n]], base, mult), [], [name])
@@ -259,14 +267,14 @@ def rank_program(g, core, T, topo):
     sts("per", "k16", 0.0, OP.mult, "tq", OP.add)
     sts("coff", "k16", "tq", OP.add)
     tt(T.pat[:], T.t1[:, 0:16], T.dg[:, 0:16], OP.add, ["t1", "dg"], ["pat"])
-    sts("qz", "qoff", -1.0, OP.mult, float(H), OP.add)
+    sts("qz", "qoff", -1.0, OP.mult, H + LEAD * U, OP.add)
     sts("qm2", "qoff2", float(H), OP.subtract)
     act(T.md[:], ind("pat", "per", 0, 16), ["pat", "per"], ["md"], scale=BIG)
-    for n, k in (("md2", BIG2 / BIG), ("md3", 1 / U)):
+    for n, k in (("md2", BIG2 / BIG), ("md3", float(ROW))):
         act(T[n][:], T.md[:], ["md"], [n], scale=k)
     for j in (1, 2):
         sts("cc%d" % j, "coff", float(j * C), OP.add)
-    sts("ck", "coff", float(2 * C), OP.add, 1 / U, OP.mult)
+    sts("ck", "coff", CELL0, OP.subtract)
     scopy("qu", "qli")
     scopy("pu", "pli")
     copy(T.qn[:].indirect(T.qu[:, 0:K]), T.cb[:], ["qu", "cb"], ["qn"])
@@ -305,7 +313,8 @@ def rank_program(g, core, T, topo):
         send(partner, T[aa][:], T[ao][:], "arA%d" % r, [ao])
         if r == 0:
             unit(2)
-        tt(block("wa", 1), ind("fs", ao), T.aw[:], OP.add, both("fs") + both("aw") + [ao], both(("wa", 1)))
+        for i, (c0, c1) in enumerate(PARTS):
+            tt(block("wa", 2 * STAGES, PARTS[i]), T.fs[:].indirect(T[ao][:, c0 // 16:c1 // 16]), T.aw[:, c0:c1], OP.add, both("fs") + both("aw") + [ao], [(("wa", 2 * STAGES), i)])
         if r == 0:
             unit(3)
 
@@ -316,15 +325,14 @@ def rank_program(g, core, T, topo):
             act(block("fa", b), ind("fh", aa, C * b, C * b + C), [("fh", b), aa], [("fa", b)])
 
         gaps = [lambda: scan("scf", "fs", 0, "md", both("fs")),
-                lambda: ts(T.t4[:], ends("scf"), T.qoff[:, 0:1], OP.is_gt, ["scf", "qoff"], ["t4"], BIG / U, OP.mult),
+                lambda: ts(T.t4[:], ends("scf"), T.qoff[:, 0:1], OP.is_gt, ["scf", "qoff"], ["t4"], BIG, OP.mult),
                 lambda: ts(T.t5[:], ends("scf"), T.qoff[:, 0:1], OP.is_gt, ["scf", "qoff"], ["t5"], float(SAME), OP.mult),
-                lambda: stt("nk", "t4", "ck", OP.add),
-                lambda: stt("fix", "t5", "coff", OP.add)]
+                lambda: stt("nk", "t4", "cc2", OP.add),
+                lambda: stt("fix", "t5", "ck", OP.add)]
         if r > 0:
             gaps += [lambda: scan("sh1", "qn", 0, "md2", ["qn"]), lambda: take("qu", "sh1")]
         else:
             gaps += mates()
-            act(T.tab[:, SAME:SAME + C], T.cb[:], ["cb"], ["same"])
 
         def gap():
             if gaps:
@@ -333,64 +341,84 @@ def rank_program(g, core, T, topo):
         def keep(b):
             act(block("fo", b), bank("pa", b), [], [("fo", b), ("pa", b)], scale=32.0 if b >= 2 else None)
 
-        def slots(buf, a):
-            return [key for j in range(a, 3) for key in both((buf, j))]
+        def slots(a, n):
+            return [key for j in range(a, a + n) for key in both(("wa", j))]
 
         for b in range(4):
             mm(("pa", b), "ec", "es", tc, tsn, [("ec", b)] + both(tc), 128 * b)
         for b in range(4):
             mm(("pb", b), "ec", "es", ac, asn, [("ec", b), ac, asn], 128 * b)
         keep(0)
-        keep(1)
-        src, at, s, before = "wa", 1, 1, 0
+        at, s, before, ahead_by = 2 * STAGES, 1, 0, LEAD
         for i in range(STAGES):
-            cur, w0, last = ("wa", "wb")[i % 2], 2 * K * (i % 2), i == STAGES - 1
-            scan("sc0", src, C * at, "md", both((src, at)))
+            w0, last = 2 * K * (i % 2), i == STAGES - 1
+            for j, part in enumerate(PARTS):
+                scan("sc0", "wa", C * at, "md", slots(at, 1) if i else [(("wa", at), j)], part, [("sc0", j)])
             if i == 0:
-                act(block(cur, 2), block(src, at), both((src, at)), both((cur, 2)), -s * U)
-                keep(2)
-                gap()
+                act(block("wa", at - 1), block("wa", at), slots(at, 1), slots(at - 1, 1), s * U)
+                keep(1)
             else:
                 c = 3 * K - w0
-                act(block(cur, 1), T[src][:].indirect(T.wu[:, c:c + K]), slots(src, 0) + [("wu", c)], both((cur, 1)), before * U)
-                ts(block(cur, 2, (0, 256)), block(src, at, (0, 256)), -s * U, OP.add, both((src, at)), [((cur, 2), 0)])
-                act(block(cur, 2, (256, C)), block(src, at, (256, C)), both((src, at)), [((cur, 2), 1)], -s * U)
-            for j in range(1 if last else 2):
-                tt(T.wu[:, w0 + K * j:w0 + K * j + K], ends("sc0"), T["cc%d" % (j + 1)][:], OP.min, ["sc0", "cc%d" % (j + 1)], [("wu", w0 + K * j)])
+                shared("wa", C * (at - 1), "wa", C * at, C * (at + 3), "wu", c, (s + before) * U, slots(at, 3) + [("wu", c)], ("wa", at - 1), 64)
+            if i == 2 and r == 0:
+                act(T.tab[:, SAME:SAME + C], T.cb[:], ["cb"], ["same"])
+            for j, part in enumerate(PARTS):
+                tt(short("wu", part, w0), ends("sc0", part), short("cc1", part), OP.min, [("sc0", j), "cc1"], [("wu", w0, j)])
+            if not last:
+                tt(T.wu[:, w0 + K:w0 + 2 * K], ends("sc0"), T.cc2[:], OP.min, both("sc0") + ["cc2"], [("wu", w0 + K)])
             gap()
-            shared(cur, 0, cur, C, 3 * C, "wu", w0, s * U, slots(cur, 1) + [("wu", w0)], (cur, 0), 1 / U if last else None)
+            ahead_by += s
+            bias = (s - ahead_by - MID if last else s) * U
+            for j, part in enumerate(PARTS):
+                out, win = block("wa", at - 2, part), T.wa[:, C * (at - 1):C * (at + 1)].indirect(short("wu", part, w0))
+                reads = slots(at - 1, 2) + [("wu", w0, j)]
+                if j == 0:
+                    act(out, win, reads, [(("wa", at - 2), j)], bias)
+                else:
+                    ts(out, win, bias, OP.add, reads, [(("wa", at - 2), j)])
             gap()
-            src, at, s, before = cur, 0, 2 * s + before, s
+            at, s, before = at - 2, 2 * s + before, s
         while gaps:
             gap()
-        scan("sc0", src, 0, "md3", both((src, 0)))
+        scan("sc0", "wa", 0, "md", slots(0, 1), (0, C), ["sc0"] + both("sc0"))
+        keep(2)
+        half(0)
+        act(T.wg[:], ends("sc0"), ["sc0"], ["wg"], ROUND)
+        half(1)
+        act(T.t1[:], T.wg[:], ["wg"], ["t1"], -ROUND)
+        half(2)
+        act(T.wg[:], T.t1[:], ["t1"], ["wg"], C - 1 - ROW * MET - CELL0, float(ROW))
+        half(3)
         keep(3)
-        for b in range(4):
-            half(b)
-        tt(T.t1[:], ends("sc0"), T.nk[:], OP.min, ["sc0", "nk"], ["t1"])
-        ts(T.wz[:], ends("sc0"), (H - 1) / 2, OP.subtract, ["sc0"], ["wz"], U, OP.mult)
-        sts("lu", "t1", (H - 1) / 2, OP.subtract, U, OP.mult)
-        sts("t3", "wz", H - 1 / U, OP.mult, float(C - H * MET), OP.add)
-        sts("wg", "wz", float(H), OP.mult, float(C - 1 - H * MET), OP.add)
-        tt(T.t2[:], ends("sc0"), T.t3[:], OP.add, ["sc0", "t3"], ["t2"])
-        copy(T.lw[:].indirect(T.lu[:, 0:K]), block(src, 0), ["lu"] + both((src, 0)), ["lw"])
-        ahead(0)
-        act(T.lg[:], ind("lw", "wz", 0, MET + C), ["lw", "wz"], ["lg"])
-        stt("k1u", "t2", "coff", OP.max)
+        ts(T.t3[:], ends("sc0"), float(ROW), OP.mult, ["sc0"], ["t3"], CELL0, OP.subtract)
+        tt(T.lu[:], ends("sc0"), T.nk[:], OP.min, ["sc0", "nk"], ["lu"])
+        copy(T.wz[:], ends("sc0"), ["sc0"], ["wz"])
+        stt("k1u", "t3", "coff", OP.max)
+        copy(T.lw[:].indirect(T.lu[:, 0:K]), block("wa", 0), ["lu"] + slots(0, 1), ["lw"])
+        for i, part in enumerate(PARTS):
+            act(block("lg", 0, part), T.lw[:].indirect(short("wz", part)), ["lw", "wz"], [("lg", i)], scale=float(ROW))
         stt("t4", "wg", "fix", OP.max)
         copy(T.tab[:, 0:SAME].indirect(T.k1u[:, 0:K]), T.cb[:], ["k1u", "cb"], ["tab"])
-        tt(T.t5[:], T.t4[:], ends("sc0"), OP.subtract, ["t4", "sc0"], ["t5"])
+        stt("t5", "t4", "t3", OP.subtract)
+        ahead(0)
+        for i, part in enumerate(PARTS):
+            scan("sc2", "lg", 0, "md3", [("lg", i)], part, [("sc2", i)] + ["sc2"] * (1 - i))
+        for i, part in enumerate(PARTS):
+            tt(short("k2u", part), ends("sc2", part), short("t5", part), OP.add, [("sc2", i), "t5"], [("k2u", i)])
+        for i, (c0, c1) in enumerate(PARTS):
+            c = (c0 + c1) // 2
+            act(T.mw[:, c:c1], T.tab[:].indirect(short("k2u", (c, c1))), ["tab", "same", ("k2u", i)], [(("mw", i), 1)])
+            copy(T.mw[:, c0:c], T.tab[:].indirect(short("k2u", (c0, c))), ["tab", "same", ("k2u", i)], [(("mw", i), 0)])
         ahead(1)
-        ahead(2)
-        scan("sc2", "lg", 0, "md3", ["lg"])
-        tt(T.k2u[:], ends("sc2"), T.t5[:], OP.add, ["sc2", "t5"], ["k2u"])
-        shared("mw", 0, "tab", 0, NCELL, "k2u", 0, None, ["tab", "same", "k2u"], "mw")
-        ahead(3)
-        scan("sh0", "mw", 0, "md2", both("mw"))
-        take(mo, "sh0")
-        send(partner, T[am][:], T[mo][:], "arM%d" % r, [mo])
-        shared("sm", 0, "ssb", 0, C, mo, 0, None, both("ssb") + [mo], "sm")
+        for i, part in enumerate(PARTS):
+            scan("sh0", "mw", 0, "md2", both(("mw", i)), part, [("sh0", i)])
+        for i, part in enumerate(PARTS):
+            ts(short(mo, part), ends("sh0", part), T.qm2[:, 0:1], OP.subtract, [("sh0", i), "qm2"], [(mo, i)])
+            send(partner, short(am, part, 4 * i), short(mo, part), "arM%d%d" % (r, i), [(mo, i)])
+        shared("sm", 0, "ssb", 0, C, mo, 0, None, both("ssb") + both(mo), "sm")
         shared("sd", 0, "sm", 0, C, "highu", 0, None, both("sm") + ["highu"], "sd")
+        ahead(2)
+        ahead(3)
         tt(T.sg[:], ind("sm", "lowu"), T.sd[:], OP.is_gt, both("sm") + both("sd") + ["lowu"], ["sg"])
         if r == 2:
             quant("vc", "vs", "vt")
@@ -399,7 +427,7 @@ def rank_program(g, core, T, topo):
 
         def travel(b, i):
             c0, c1 = PARTS[i]
-            tt(T.zt[:, 4 * c0 + b:4 * c1:4], block("fh", b).indirect(T[am][:, c0 // 16:c1 // 16]), block("fa", b, PARTS[i]), OP.add, [("fh", b), ("fa", b), am], [("zt", b, i)])
+            tt(T.zt[:, 4 * c0 + b:4 * c1:4], block("fh", b).indirect(short(am, PARTS[i], 4 * i)), block("fa", b, PARTS[i]), OP.add, [("fh", b), ("fa", b), (am, i)], [("zt", b, i)])
 
         def layer(i, order):
             quant_part(zc, zs, "zt", i, [("zt", b, i) for b in range(4)])
@@ -416,17 +444,17 @@ def rank_program(g, core, T, topo):
 
         def turn(b, part, keys):
             c0, c1 = part
-            act(T.xn[:, 4 * c0 + b:4 * c1:4], block("y3", b).indirect(T[mo][:, c0 // 16:c1 // 16]), both(("y3", b)) + [mo], keys, scale=0.03125)
+            act(T.xn[:, 4 * c0 + b:4 * c1:4], block("y3", b).indirect(T[mo][:, c0 // 16:c1 // 16]), both(("y3", b)) + both(mo), keys, scale=0.03125)
 
         def late(b, part, keys):
             c0, c1 = part
-            tt(T.xn[:, 4 * c0 + b:4 * c1:4], block("rs", b).indirect(T[mo][:, c0 // 16:c1 // 16]), block("fo", b, part), OP.add, both(("rs", b)) + [mo, ("fo", b)], keys)
+            tt(T.xn[:, 4 * c0 + b:4 * c1:4], block("rs", b).indirect(T[mo][:, c0 // 16:c1 // 16]), block("fo", b, part), OP.add, both(("rs", b)) + both(mo) + [("fo", b)], keys)
 
         def state(i):
             quant_part("tc%d" % (r + 1), "ts%d" % (r + 1), "xn", i, [(("xn", b), i) for b in range(4)])
 
         for b in (2, 3):
-            act(block("fm", b), ind("fo", mo, C * b, C * b + C), [("fo", b), mo], [("fm", b)])
+            act(block("fm", b), ind("fo", mo, C * b, C * b + C), [("fo", b)] + both(mo), [("fm", b)])
         travel(0, 0)
         stt("sgu", "t3", "tgt", OP.add)
         travel(1, 0)
@@ -455,9 +483,11 @@ def rank_program(g, core, T, topo):
         early(3, 1)
         scaled(1, 1)
         if r < 2:
-            for b in range(2):
-                turn(2 + b, (0, C), both(("xn", 2 + b)))
-                late(b, (0, C), both(("xn", b)))
+            turn(2, (0, C), both(("xn", 2)))
+            late(0, (0, C), both(("xn", 0)))
+            for i, part in enumerate(PARTS):
+                turn(3, part, [(("xn", 3), i)])
+                late(1, part, [(("xn", 1), i)])
             state(0)
             state(1)
             scan("sc2", "aw", 0, "md", both("aw"))

from concourse.mybir import dt, AluOpType as OP, ActivationFunctionType as AF

C = 320
K = C // 16
H = C // 2
STEP = [1, 2, 4]
STAGES = 6
ROW = 164
U = 1.0 / ROW
LEAD, MID = -59, (H - 1) / 2
MET = 3 * C
BIG, BIG2 = 2048.0, 512.0
ROUND = 1.5 * 2 ** 23
CELL0 = ROW * MET - MID - C
SAME = C + ROW * C
NCELL = SAME + C
PARTS = [(0, 192), (192, C)]


def wide(d, *names):
    return {n: ("sbuf", [128, C], d) for n in names}


def small(d, *names):
    return {n: ("sbuf", [128, K], d) for n in names}


def column(d, *names):
    return {n: ("sbuf", [128, 1], d) for n in names}


def tiles(*names):
    return {n: ("sbuf", [128, 4 * C], "bfloat16") for n in names}


def codes(n, *pairs):
    d = {}
    for c, s in pairs:
        d[c] = ("sbuf", [128, n], "float8_e4m3fn_x4")
        d[s] = ("sbuf", [128, n], "uint8")
    return d


SCRATCH = {
    **tiles("x0", "xn", "zt", "fo", "fh", "fa", "fm", "y3"),
    "ut": ("sbuf", [128, 512], "bfloat16"), "vt": ("sbuf", [128, 512], "bfloat16"),
    **codes(128, ("uc", "us"), ("urc", "urs"), ("vc", "vs")), **codes(512, ("lc", "ls"), ("ec", "es")),
    **codes(C, *[("zc%d" % r, "zs%d" % r) for r in range(3)], *[("ac%d" % r, "as%d" % r) for r in range(3)], *[("tc%d" % r, "ts%d" % r) for r in range(4)]),
    "ebase": ("sbuf", [128, 516], "bfloat16"),
    "ji": ("sbuf", [128, 24], "int32"), "dg": ("sbuf", [128, 24], "float32"), "pat": ("sbuf", [128, 16], "float32"),
    "u8i": ("sbuf", [128, 8], "int32"), "upick": ("sbuf", [128, 8], "uint16"),
    **column("int32", "pi1", "pa1"), **column("float32", "qoff", "qoff2", "qz", "qm2", "tq"),
    **small("int32", "pli", "qli", "mli", "k16"),
    **small("uint16", "pu", "lowu", "highu", "qu", "lu", "k1u", "k2u", "sgu", "wz", "per"),
    **small("uint16", *["%s%d" % (n, r) for n in ("aa", "mo", "ao") for r in range(3)]),
    **{"am%d" % r: ("sbuf", [128, K + 4], "uint16") for r in range(3)},
    **small("float32", "coff", "cc1", "cc2", "ck", "dmu", "tgt", "nk", "fix", "wg", "t1", "t2", "t3", "t4", "t5"),
    "wu": ("sbuf", [128, 4 * K], "uint16"),
    **wide("bfloat16", "fs", "cb", "mw", "sg", "sgw", "qs", "qn", "scf", "md", "md2", "md3"), **wide("float16", "sh0", "sh1"),
    **wide("float32", "aw", "lg", "ssb", "sc0", "sc2", "sm", "sd"),
    "wa": ("sbuf", [128, (2 * STAGES + 1) * C], "float32"),
    "lw": ("sbuf", [128, MET + C], "float32"), "tab": ("sbuf", [128, NCELL], "bfloat16"),
    "rs": ("sbuf", [128, 4 * C], "float32"),
    "pa": ("psum", [128, 2048], "float32"), "pb": ("psum", [128, 2048], "float32"),
}

LOADS = (("x0", 16), ("x1", 16), ("u", 16), ("v", 16), ("wc", 16), ("ws", 16), ("pl", 16), ("ql", 16), ("ml", 16))
SEMAPHORES = ["qV", "qS", "qT", "qG", "sent", "stored"] + ["ld_" + n for n, _ in LOADS]
for _r in range(3):
    SEMAPHORES += ["arX%d" % _r, "arA%d" % _r, "arM%d0" % _r, "arM%d1" % _r]


def make_queues(g, T):
    queues = {"V": g.vector, "S": g.scalar, "T": g.tensor, "G": g, "Y": g.sync}
    count = {"V": 0, "S": 0, "T": 0, "G": 0}
    clocks = {}
    known = {q: {} for q in queues}
    writer, readers = {}, {}

    def merge(a, b):
        for k, n in b.items():
            if a.get(k, 0) < n:
                a[k] = n

    def need(q, sem, n):
        if known[q].get(sem, 0) >= n:
            return
        queues[q].wait_ge(T.sem[sem], n)
        if (sem, n) in clocks:
            merge(known[q], clocks[(sem, n)])
        known[q][sem] = n

    def waits(q, reads, writes):
        own = "q" + q
        want = {}
        for k in reads:
            if k in writer:
                s, n = writer[k]
                want[s] = max(want.get(s, 0), n)
        for k in writes:
            if k in writer:
                s, n = writer[k]
                want[s] = max(want.get(s, 0), n)
            for s, n in readers.get(k, {}).items():
                if s != own:
                    want[s] = max(want.get(s, 0), n)
        for s, n in want.items():
            need(q, s, n)

    def note(sem, n, reads, writes):
        for k in reads:
            r = readers.setdefault(k, {})
            r[sem] = max(r.get(sem, 0), n)
        for k in writes:
            writer[k] = (sem, n)
            readers[k] = {}

    def op(q, fn, reads, writes):
        waits(q, reads, writes)
        inst = fn(queues[q])
        count[q] += 1
        sem = "q" + q
        inst.then_inc(T.sem[sem], 1)
        c = dict(known[q])
        merge(c, clocks.get((sem, count[q] - 1), {}))
        c[sem] = count[q]
        clocks[(sem, count[q])] = c
        note(sem, count[q], reads, writes)

    def dma(q, pairs, sem, total, reads, writes):
        waits(q, reads, writes)
        for out, in_ in pairs:
            queues[q].dma_start(out, in_).then_inc(T.sem[sem], 16)
        note(sem, total, reads, writes)

    def arrives(sem, total, writes):
        note(sem, total, [], writes)

    return op, dma, arrives, waits, need, count


def rank_program(g, core, T, topo):
    rank = T.rank_of(core)
    if rank is None:
        return
    op, dma, arrives, waits, need, count = make_queues(g, T)
    sent = [0]

    def send(dst, out, in_, sem, keys):
        waits("G", keys, [])
        rid, pid, _ = topo.addr(dst)
        g.remote_dma(out, in_, T.sem[sem], T.sem.sent, pid, rid, topo.mask(core, dst))
        sent[0] += len(topo.engines(core, dst))

    def act(out, in_, reads, writes, bias=None, scale=None):
        if bias is not None:
            op("S", lambda e: e.activation(out, in_, AF.Identity, bias, 1.0 if scale is None else scale), reads, writes)
        elif scale is not None:
            op("S", lambda e: e.activation(out, in_, AF.Copy, 0.0, scale), reads, writes)
        else:
            op("S", lambda e: e.activation(out, in_, AF.Copy), reads, writes)

    def copy(out, in_, reads, writes):
        op("V", lambda e: e.tensor_copy(out, in_), reads, writes)

    def tt(out, a, b, o, reads, writes):
        op("V", lambda e: e.tensor_tensor(out, a, b, o), reads, writes)

    def ts(out, a, s1, o1, reads, writes, s2=None, o2=None):
        if o2 is None:
            op("V", lambda e: e.tensor_scalar(out, a, s1, None, o1), reads, writes)
        else:
            op("V", lambda e: e.tensor_scalar(out, a, s1, s2, o1, o2), reads, writes)

    def stt(out, a, b, o):
        tt(T[out][:], T[a][:], T[b][:], o, [a, b], [out])

    def sts(out, a, s1, o1, s2=None, o2=None):
        cols = [s for s in (s1, s2) if isinstance(s, str)]
        s1, s2 = [T[s][:, 0:1] if isinstance(s, str) else s for s in (s1, s2)]
        ts(T[out][:], T[a][:], s1, o1, [a] + cols, [out], s2, o2)

    def scopy(out, a):
        copy(T[out][:], T[a][:], [a], [out])

    def ind(win, off, a=0, b=C):
        return T[win][:, a:b].indirect(T[off][:, 0:K])

    def both(key):
        return [(key, 0), (key, 1)]

    def shared(out, o, win, a, b, off, c, bias, reads, key, n=H):
        v, s = [T[win][:, a:b].indirect(T[off][:, c + c0 // 16:c + c1 // 16]) for c0, c1 in ((0, n), (n, C))]
        act(T[out][:, o + n:o + C], s, reads, [(key, 1)], bias)
        if bias is None:
            copy(T[out][:, o:o + n], v, reads, [(key, 0)])
        else:
            ts(T[out][:, o:o + n], v, bias, OP.add, reads, [(key, 0)])

    def scan(dst, src, a, jump, reads, part=(0, C), keys=None):
        c0, c1 = part
        op("V", lambda e: e.tensor_tensor_scan(T[dst][:, c0:c1], T[jump][:, c0:c1], T[src][:, a + c0:a + c1], 0.0, OP.add, OP.max), [jump] + reads, keys or [dst])

    def ends(sc, part=(0, C)):
        return T[sc][:, part[0] + 15:part[1]:16]

    def short(name, part, c=0):
        return T[name][:, c + part[0] // 16:c + part[1] // 16]

    def take(out, sc):
        ts(T[out][:], ends(sc), T.qm2[:, 0:1], OP.subtract, [sc, "qm2"], [out])

    def mm(bank, lc, ls, rc, rs, reads, a, part=(0, C)):
        (buf, b), (c0, c1) = bank, part
        op("T", lambda e: e.matmul_mx(T[buf][:, 512 * b:512 * b + c1 - c0], T[lc][:, a:a + 128], T[ls][:, a:a + 128], T[rc][:, c0:c1], T[rs][:, c0:c1], True, True), reads, [(buf, b)])

    def bank(buf, b, part=(0, C)):
        return T[buf][:, 512 * b:512 * b + part[1] - part[0]]

    def block(buf, b, part=(0, C)):
        return T[buf][:, C * b + part[0]:C * b + part[1]]

    def quant(c, s, t):
        op("V", lambda e: e.quantize_mx(T[c][:], T[s][:], T[t][:]), [t], [c, s])

    def quant_part(c, s, t, i, reads):
        c0, c1 = PARTS[i]
        op("V", lambda e: e.quantize_mx(T[c][:, c0:c1], T[s][:, c0:c1], T[t][:, 4 * c0:4 * c1]), reads, [(c, i)])

    def unit(b):
        op("V", lambda e: e.quantize_mx(T.ec[:, 128 * b:128 * b + 128], T.es[:, 128 * b:128 * b + 128], T.ebase[:, 3 - b:515 - b]), ["ebase"], [("ec", b)])

    dma("S", [(T.ut[:], T.u[:])], "ld_u", 16, [], ["ut"])
    for i, (c0, c1) in enumerate(PARTS):
        dma("S", [(T.x0[:, 4 * c0:4 * c1], T.x[:, 4 * c0:4 * c1])], "ld_x%d" % i, 16, [], [("x0", i)])
    dma("Y", [(T.qli[:], T.ql[:])], "ld_ql", 16, [], ["qli"])
    dma("Y", [(T.pli[:], T.pl[:])], "ld_pl", 16, [], ["pli"])
    need("Y", "ld_x1", 16)
    dma("Y", [(T.mli[:], T.ml[:])], "ld_ml", 16, [], ["mli"])
    dma("Y", [(T.lc[:].bitcast(dt.uint8), T.wc[:])], "ld_wc", 16, [], ["lc"])
    dma("Y", [(T.ls[:], T.ws[:])], "ld_ws", 16, [], ["ls"])
    dma("Y", [(T.vt[:], T.v[:])], "ld_v", 16, [], ["vt"])
    for r in range(3):
        e = len(topo.engines(T.cores[rank ^ STEP[r]], core))
        arrives("arX%d" % r, 2 * e, ["ac%d" % r, "as%d" % r])
        arrives("arA%d" % r, e, ["aa%d" % r])
        for i in range(2):
            arrives("arM%d%d" % (r, i), e, [("am%d" % r, i)])

    def iota(name, n, step, base, mult, flag=False):
        op("G", lambda e: e.iota(T[name][:], [[step, n]], base, mult, allow_small_or_imprecise_dtypes=True) if flag else e.iota(T[name][:], [[step, n]], base, mult), [], [name])
    iota("pi1", 1, 1, 0, 1)
    iota("ji", 24, 1, 4095, -1)
    iota("u8i", 8, 16, 0, 0)
    iota("k16", K, 16, 0, 0)
    iota("cb", C, 1, -H, 0, True)
    op("V", lambda e: e.memset(T.ebase[:], 1.0), [], ["ebase"])
    op("G", lambda e: e.affine_select(T.ebase[:], T.ebase[:], [[-1, 516]], OP.is_equal, 0.0, 3, 4), ["ebase"], ["ebase"])
    sts("pa1", "pi1", 15, OP.bitwise_and)
    sts("ji", "ji", 15, OP.bitwise_and)
    scopy("tq", "pa1")
    sts("qoff", "pa1", 15.0, OP.is_lt, BIG, OP.mult)
    sts("dg", "ji", 0.0, OP.is_equal)
    sts("qoff2", "pa1", 15.0, OP.is_lt, BIG2, OP.mult)
    scopy("upick", "u8i")
    ts(T.t1[:, 0:16], T.dg[:, 1:17], -3.0, OP.mult, ["dg"], ["t1"])
    sts("per", "k16", 0.0, OP.mult, "tq", OP.add)
    sts("coff", "k16", "tq", OP.add)
    tt(T.pat[:], T.t1[:, 0:16], T.dg[:, 0:16], OP.add, ["t1", "dg"], ["pat"])
    sts("qz", "qoff", -1.0, OP.mult, H + LEAD * U, OP.add)
    sts("qm2", "qoff2", float(H), OP.subtract)
    act(T.md[:], ind("pat", "per", 0, 16), ["pat", "per"], ["md"], scale=BIG)
    for n, k in (("md2", BIG2 / BIG), ("md3", float(ROW))):
        act(T[n][:], T.md[:], ["md"], [n], scale=k)
    for j in (1, 2):
        sts("cc%d" % j, "coff", float(j * C), OP.add)
    sts("ck", "coff", CELL0, OP.subtract)
    scopy("qu", "qli")
    scopy("pu", "pli")
    copy(T.qn[:].indirect(T.qu[:, 0:K]), T.cb[:], ["qu", "cb"], ["qn"])
    quant("uc", "us", "ut")
    unit(0)
    act(T.aw[:], ind("qn", "pu"), ["qn", "pu", "qz"], both("aw"), T.qz[:, 0:1])
    op("S", lambda e: e.activation(T.urs[:], T.us[:].indirect(T.upick[:, 0:8]), AF.Copy), ["us", "upick"], ["urs"])
    op("V", lambda e: e.tensor_copy(T.urc[:].bitcast(dt.uint32), T.uc[:].bitcast(dt.uint32).indirect(T.upick[:, 0:8])), ["uc", "upick"], ["urc"])
    scan("sc2", "aw", 0, "md", both("aw"))
    quant_part("tc0", "ts0", "x0", 0, [("x0", 0)])
    copy(T.ao0[:], ends("sc2"), ["sc2"], ["ao0"])
    quant_part("tc0", "ts0", "x0", 1, [("x0", 1)])
    unit(1)

    def mates():
        return [lambda: stt("t1", "mli", "coff", OP.min),
                lambda: stt("t2", "mli", "coff", OP.max),
                lambda: stt("dmu", "mli", "coff", OP.subtract),
                lambda: scopy("lowu", "t1"),
                lambda: scopy("highu", "t2"),
                lambda: sts("t3", "dmu", "qoff2", OP.mult),
                lambda: stt("tgt", "coff", "t3", OP.subtract)]

    for r in range(3):
        partner = T.cores[rank ^ STEP[r]]
        tc, tsn, zc, zs = "tc%d" % r, "ts%d" % r, "zc%d" % r, "zs%d" % r
        ao, mo, aa, am, ac, asn = "ao%d" % r, "mo%d" % r, "aa%d" % r, "am%d" % r, "ac%d" % r, "as%d" % r
        send(partner, T[ac][:].bitcast(dt.uint8), T[tc][:].bitcast(dt.uint8), "arX%d" % r, both(tc))
        send(partner, T[asn][:], T[tsn][:], "arX%d" % r, both(tc))
        for i, part in enumerate(PARTS):
            mm(("pb", i), "urc", "urs", tc, tsn, ["urc", "urs", (tc, i)], 0, part)
            ts(block("fs", 0, part), bank("pb", i, part), 0.0, OP.is_lt, [], [("fs", i), ("pb", i)], float(MET), OP.mult)
            act(block("ssb", 0, part), bank("pb", i, part), [], [("ssb", i), ("pb", i)])
            if i == 0 and r > 0:
                copy(T[ao][:], ends("sc2"), ["sc2"], [ao])
        send(partner, T[aa][:], T[ao][:], "arA%d" % r, [ao])
        if r == 0:
            unit(2)
        for i, (c0, c1) in enumerate(PARTS):
            tt(block("wa", 2 * STAGES, PARTS[i]), T.fs[:].indirect(T[ao][:, c0 // 16:c1 // 16]), T.aw[:, c0:c1], OP.add, both("fs") + both("aw") + [ao], [(("wa", 2 * STAGES), i)])
        if r == 0:
            unit(3)

        def half(b):
            act(block("fh", b), bank("pb", b), [], [("fh", b), ("pb", b)], scale=0.5)

        def ahead(b):
            act(block("fa", b), ind("fh", aa, C * b, C * b + C), [("fh", b), aa], [("fa", b)])

        gaps = [lambda: scan("scf", "fs", 0, "md", both("fs")),
                lambda: ts(T.t4[:], ends("scf"), T.qoff[:, 0:1], OP.is_gt, ["scf", "qoff"], ["t4"], BIG, OP.mult),
                lambda: ts(T.t5[:], ends("scf"), T.qoff[:, 0:1], OP.is_gt, ["scf", "qoff"], ["t5"], float(SAME), OP.mult),
                lambda: stt("nk", "t4", "cc2", OP.add),
                lambda: stt("fix", "t5", "ck", OP.add)]
        if r > 0:
            gaps += [lambda: scan("sh1", "qn", 0, "md2", ["qn"]), lambda: take("qu", "sh1")]
        else:
            gaps += mates()

        def gap():
            if gaps:
                gaps.pop(0)()

        def keep(b):
            act(block("fo", b), bank("pa", b), [], [("fo", b), ("pa", b)], scale=32.0 if b >= 2 else None)

        def slots(a, n):
            return [key for j in range(a, a + n) for key in both(("wa", j))]

        for b in range(4):
            mm(("pa", b), "ec", "es", tc, tsn, [("ec", b)] + both(tc), 128 * b)
        for b in range(4):
            mm(("pb", b), "ec", "es", ac, asn, [("ec", b), ac, asn], 128 * b)
        keep(0)
        at, s, before, ahead_by = 2 * STAGES, 1, 0, LEAD
        for i in range(STAGES):
            w0, last = 2 * K * (i % 2), i == STAGES - 1
            for j, part in enumerate(PARTS):
                scan("sc0", "wa", C * at, "md", slots(at, 1) if i else [(("wa", at), j)], part, [("sc0", j)])
            if i == 0:
                act(block("wa", at - 1), block("wa", at), slots(at, 1), slots(at - 1, 1), s * U)
                keep(1)
            else:
                c = 3 * K - w0
                shared("wa", C * (at - 1), "wa", C * at, C * (at + 3), "wu", c, (s + before) * U, slots(at, 3) + [("wu", c)], ("wa", at - 1), 64)
            if i == 2 and r == 0:
                act(T.tab[:, SAME:SAME + C], T.cb[:], ["cb"], ["same"])
            for j, part in enumerate(PARTS):
                tt(short("wu", part, w0), ends("sc0", part), short("cc1", part), OP.min, [("sc0", j), "cc1"], [("wu", w0, j)])
            if not last:
                tt(T.wu[:, w0 + K:w0 + 2 * K], ends("sc0"), T.cc2[:], OP.min, both("sc0") + ["cc2"], [("wu", w0 + K)])
            gap()
            ahead_by += s
            bias = (s - ahead_by - MID if last else s) * U
            for j, part in enumerate(PARTS):
                out, win = block("wa", at - 2, part), T.wa[:, C * (at - 1):C * (at + 1)].indirect(short("wu", part, w0))
                reads = slots(at - 1, 2) + [("wu", w0, j)]
                if j == 0:
                    act(out, win, reads, [(("wa", at - 2), j)], bias)
                else:
                    ts(out, win, bias, OP.add, reads, [(("wa", at - 2), j)])
            gap()
            at, s, before = at - 2, 2 * s + before, s
        while gaps:
            gap()
        scan("sc0", "wa", 0, "md", slots(0, 1), (0, C), ["sc0"] + both("sc0"))
        keep(2)
        half(0)
        act(T.wg[:], ends("sc0"), ["sc0"], ["wg"], ROUND)
        half(1)
        act(T.t1[:], T.wg[:], ["wg"], ["t1"], -ROUND)
        half(2)
        act(T.wg[:], T.t1[:], ["t1"], ["wg"], C - 1 - ROW * MET - CELL0, float(ROW))
        half(3)
        keep(3)
        ts(T.t3[:], ends("sc0"), float(ROW), OP.mult, ["sc0"], ["t3"], CELL0, OP.subtract)
        tt(T.lu[:], ends("sc0"), T.nk[:], OP.min, ["sc0", "nk"], ["lu"])
        copy(T.wz[:], ends("sc0"), ["sc0"], ["wz"])
        stt("k1u", "t3", "coff", OP.max)
        copy(T.lw[:].indirect(T.lu[:, 0:K]), block("wa", 0), ["lu"] + slots(0, 1), ["lw"])
        for i, part in enumerate(PARTS):
            act(block("lg", 0, part), T.lw[:].indirect(short("wz", part)), ["lw", "wz"], [("lg", i)], scale=float(ROW))
        stt("t4", "wg", "fix", OP.max)
        copy(T.tab[:, 0:SAME].indirect(T.k1u[:, 0:K]), T.cb[:], ["k1u", "cb"], ["tab"])
        stt("t5", "t4", "t3", OP.subtract)
        ahead(0)
        for i, part in enumerate(PARTS):
            scan("sc2", "lg", 0, "md3", [("lg", i)], part, [("sc2", i)] + ["sc2"] * (1 - i))
        for i, part in enumerate(PARTS):
            tt(short("k2u", part), ends("sc2", part), short("t5", part), OP.add, [("sc2", i), "t5"], [("k2u", i)])
        for i, (c0, c1) in enumerate(PARTS):
            c = (c0 + c1) // 2
            act(T.mw[:, c:c1], T.tab[:].indirect(short("k2u", (c, c1))), ["tab", "same", ("k2u", i)], [(("mw", i), 1)])
            copy(T.mw[:, c0:c], T.tab[:].indirect(short("k2u", (c0, c))), ["tab", "same", ("k2u", i)], [(("mw", i), 0)])
        ahead(1)
        for i, part in enumerate(PARTS):
            scan("sh0", "mw", 0, "md2", both(("mw", i)), part, [("sh0", i)])
        for i, part in enumerate(PARTS):
            ts(short(mo, part), ends("sh0", part), T.qm2[:, 0:1], OP.subtract, [("sh0", i), "qm2"], [(mo, i)])
            send(partner, short(am, part, 4 * i), short(mo, part), "arM%d%d" % (r, i), [(mo, i)])
        shared("sm", 0, "ssb", 0, C, mo, 0, None, both("ssb") + both(mo), "sm")
        shared("sd", 0, "sm", 0, C, "highu", 0, None, both("sm") + ["highu"], "sd")
        ahead(2)
        ahead(3)
        tt(T.sg[:], ind("sm", "lowu"), T.sd[:], OP.is_gt, both("sm") + both("sd") + ["lowu"], ["sg"])
        if r == 2:
            quant("vc", "vs", "vt")
        scan("sh1", "sg", 0, "md2", ["sg"])
        tt(T.t3[:], ends("sh1"), T.dmu[:], OP.mult, ["sh1", "dmu"], ["t3"])

        def travel(b, i):
            c0, c1 = PARTS[i]
            tt(T.zt[:, 4 * c0 + b:4 * c1:4], block("fh", b).indirect(short(am, PARTS[i], 4 * i)), block("fa", b, PARTS[i]), OP.add, [("fh", b), ("fa", b), (am, i)], [("zt", b, i)])

        def layer(i, order):
            quant_part(zc, zs, "zt", i, [("zt", b, i) for b in range(4)])
            for b in order:
                mm((("pa", "pb")[i], b), "lc", "ls", zc, zs, ["lc", "ls", (zc, i)], 128 * b, PARTS[i])

        def early(b, i):
            buf = ("pa", "pb")[i]
            tt(block("y3", b, PARTS[i]), bank(buf, b, PARTS[i]), block("fm", b, PARTS[i]), OP.add, [("fm", b)], [(("y3", b), i), (buf, b)])

        def scaled(b, i):
            buf = ("pa", "pb")[i]
            act(block("rs", b, PARTS[i]), bank(buf, b, PARTS[i]), [], [(("rs", b), i), (buf, b)], scale=0.03125)

        def turn(b, part, keys):
            c0, c1 = part
            act(T.xn[:, 4 * c0 + b:4 * c1:4], block("y3", b).indirect(T[mo][:, c0 // 16:c1 // 16]), both(("y3", b)) + both(mo), keys, scale=0.03125)

        def late(b, part, keys):
            c0, c1 = part
            tt(T.xn[:, 4 * c0 + b:4 * c1:4], block("rs", b).indirect(T[mo][:, c0 // 16:c1 // 16]), block("fo", b, part), OP.add, both(("rs", b)) + both(mo) + [("fo", b)], keys)

        def state(i):
            quant_part("tc%d" % (r + 1), "ts%d" % (r + 1), "xn", i, [(("xn", b), i) for b in range(4)])

        for b in (2, 3):
            act(block("fm", b), ind("fo", mo, C * b, C * b + C), [("fo", b)] + both(mo), [("fm", b)])
        travel(0, 0)
        stt("sgu", "t3", "tgt", OP.add)
        travel(1, 0)
        act(T.sgw[:], ind("cb", "sgu"), ["cb", "sgu"], ["sgw"])
        act(T.qs[:], ind("sgw", "qu"), ["sgw", "qu"], ["qs"])
        travel(2, 0)
        travel(3, 0)
        travel(0, 1)
        layer(0, (2, 3, 0, 1))
        for b in (1, 2, 3):
            travel(b, 1)
        if r < 2:
            act(T.qn[:], ind("qs", "sgu"), ["qs", "sgu"], ["qn"])
        else:
            act(T.lg[:], ind("qs", "sgu"), ["qs", "sgu"], ["lg"], float(H))
            dma("Y", [(T.qo[:], T.lg[0:128:16, :])], "stored", 16, ["lg"], [])
        scaled(0, 0)
        scaled(1, 0)
        early(2, 0)
        layer(1, (2, 0, 3, 1))
        early(3, 0)
        if r < 2:
            shared("aw", 0, "qn", 0, C, "pu", 0, T.qz[:, 0:1], ["qn", "pu"], "aw")
        early(2, 1)
        scaled(0, 1)
        early(3, 1)
        scaled(1, 1)
        if r < 2:
            turn(2, (0, C), both(("xn", 2)))
            late(0, (0, C), both(("xn", 0)))
            for i, part in enumerate(PARTS):
                turn(3, part, [(("xn", 3), i)])
                late(1, part, [(("xn", 1), i)])
            state(0)
            state(1)
            scan("sc2", "aw", 0, "md", both("aw"))
        else:
            for i, part in enumerate(PARTS):
                for b in range(2):
                    turn(2 + b, part, [(("xn", 2 + b), i)])
                    late(b, part, [(("xn", b), i)])
                    if (i, b) == (1, 0):
                        state(0)
            state(1)
    for i, (c0, c1) in enumerate(PARTS):
        mm(("pb", i), "vc", "vs", "tc3", "ts3", ["vc", "vs", ("tc3", i)], 0, PARTS[i])
        dma("Y", [(T.oc[:, 4 * c0:4 * c1], T.tc3[:, c0:c1].bitcast(dt.uint8))], "stored", 32 + 16 * i, [("tc3", i)], [])
    act(block("sc0", 0, PARTS[0]), bank("pb", 0, PARTS[0]), [], ["sc0", ("pb", 0)])
    dma("S", [(block("y", 0, PARTS[0]), block("sc0", 0, PARTS[0]))], "stored", 64, ["sc0"], [])
    copy(block("sc2", 0, PARTS[1]), bank("pb", 1, PARTS[1]), [], ["sc2", ("pb", 1)])
    dma("Y", [(T.osc[4 * k:4 * k + 4, :], T.ts3[32 * k:32 * k + 4, :]) for k in range(4)], "stored", 128, both("tc3"), [])
    dma("S", [(block("y", 0, PARTS[1]), block("sc2", 0, PARTS[1]))], "stored", 144, ["sc2"], [])
    g.sync.wait_ge(T.sem.stored, 144)
    g.wait_ge(T.sem.sent, sent[0])
    for q in ("V", "S", "T", "G"):
        need("G", "q" + q, count[q])
    for n, t in LOADS:
        need("G", "ld_" + n, t)
